import numpy as np
import ml_dtypes


def mxq(x, axis, fmt="e4m3"):
    dtype, down = {"e4m3": (ml_dtypes.float8_e4m3fn, 7), "e5m2": (ml_dtypes.float8_e5m2, 14)}[fmt]
    v = np.moveaxis(np.asarray(x, np.float32).astype(ml_dtypes.bfloat16).astype(np.float64), axis, -1)
    blocks = v.reshape(v.shape[:-1] + (-1, 32))
    amax = np.abs(blocks).max(-1, keepdims=True)
    byte = np.maximum(np.where(amax > 0, np.frexp(amax)[1] - 1 + 127, 0) - down, 1)
    scale = np.exp2(byte - 127.0)
    codes = (blocks / scale).astype(np.float32).astype(dtype).astype(np.float64)
    return np.moveaxis((codes * scale).reshape(v.shape), -1, axis)


WIDE = False


def mx_kscale(k):
    if not WIDE:
        return np.ones(k)
    levels = np.array([10, -10, 5, -5, 0])
    if k % 512:
        return np.exp2(np.random.permutation(np.resize(levels, k // 32))).repeat(32)
    a = np.empty((k // 512, 16))
    for p in range(k // 512):
        a[p, :8] = np.random.permutation(np.resize(levels, 8))
        for g in range(8):
            far = levels[np.abs(levels - a[p, g]) >= 10]
            a[p, g + 8] = far[np.random.randint(len(far))]
    return np.exp2(a.ravel()).repeat(32)


def f64(x):
    return np.asarray(x).astype(np.float64)


def striped(idx):
    return np.tile(idx.reshape(-1, 16).T, (8, 1)).astype(np.uint16)


def unstriped(offs):
    return offs[:16].T.reshape(-1).astype(np.int64)


E2M1 = np.array([0.0, 0.5, 1.0, 1.5, 2.0, 3.0, 4.0, 6.0, -0.0, -0.5, -1.0, -1.5, -2.0, -3.0, -4.0, -6.0])


def pack_weight(w, fmt):
    k, n = w.shape
    w = f64(np.asarray(w, np.float32).astype(ml_dtypes.bfloat16)).reshape(k // 32, 32, n)
    amax = np.abs(w).max(1)
    if fmt == "e4m3":
        byte = np.frexp(amax)[1] - 1 + 127 - 7
    else:
        mant, ex = np.frexp(amax / 6.0)
        byte = np.where(mant > 0.5, ex, ex - 1) + 127
    byte = np.clip(np.where(amax > 0, byte, 1), 1, 254)
    scaled = (w * np.exp2(127.0 - byte)[:, None, :]).reshape(k, n).astype(np.float32)
    by_word = np.ascontiguousarray(scaled.reshape(k // 512, 128, 4, n).transpose(0, 1, 3, 2))
    if fmt == "e4m3":
        words = by_word.astype(ml_dtypes.float8_e4m3fn).view(np.uint8)
    else:
        c = by_word.astype(ml_dtypes.float4_e2m1fn).view(np.uint8) & 0xF
        words = (c[..., 0::2] | (c[..., 1::2] << 4)).reshape(k // 512, 128, 2 * n)
    return np.ascontiguousarray(words), np.ascontiguousarray(byte.astype(np.uint8).reshape(k // 512, 16, n))


def unpack_weight(words, scales, fmt):
    g, _, n = scales.shape
    words = np.ascontiguousarray(words).reshape(g, 128, n, -1)
    if fmt == "e4m3":
        vals = words.view(ml_dtypes.float8_e4m3fn).astype(np.float64)
    else:
        nib = np.empty((g, 128, n, 4), np.uint8)
        nib[..., 0::2] = words & 0xF
        nib[..., 1::2] = words >> 4
        vals = E2M1[nib]
    vals = vals * np.repeat(np.exp2(scales.astype(np.float64) - 127.0), 8, axis=1)[..., None]
    return vals.transpose(0, 1, 3, 2).reshape(g * 512, n)


def gelu(v):
    return 0.5 * v * (1.0 + np.tanh(np.sqrt(2.0 / np.pi) * (v + 0.044715 * v**3)))


K, H, N, T, S, T2, P = 1024, 1024, 512, 4096, 1024, 2048, 512

def setup_inputs():
    n = np.random.standard_normal
    s = mx_kscale(K)[:, None]
    u = mx_kscale(H)[:, None]
    tab_words, tab_scales = pack_weight(n((K, T)) * s, "e4m3")
    w4_words, w4_scales = pack_weight(n((H, N)) / u / np.sqrt(H), "e2m1")
    perm = np.random.permutation(T2)
    return {
        "tab_words": tab_words, "tab_scales": tab_scales,
        "offs": striped(np.random.permutation(T)[:S]),
        "w1": (1.3 * n((K, H)) / s / np.sqrt(K)).astype(np.float32),
        "cond": (0.8 * n((H, S))).astype(np.float32),
        "gain": (1.3 * np.exp(0.3 * n(H)) * u[:, 0]).astype(np.float32),
        "page0": (n((H, T2)) * u).astype(np.float32),
        "wgs": np.exp(0.3 * n((128, S))).astype(np.float32),
        "offs2": striped(np.random.permutation(T2)[:S]),
        "offs3": striped(perm[:P]), "offs4": striped(perm[P:2 * P]),
        "back": (0.8 * np.exp(0.3 * n(H))).astype(np.float32),
        "w4_words": w4_words, "w4_scales": w4_scales,
    }

def reference(tab_words, tab_scales, offs, w1, cond, gain, page0, wgs, offs2, offs3, offs4, back, w4_words, w4_scales):
    v = unpack_weight(tab_words, tab_scales, "e4m3")[:, unstriped(offs)]
    w4 = unpack_weight(w4_words, w4_scales, "e2m1")
    pre = (mxq(f64(w1), 0, "e4m3").T @ v) + f64(cond)
    h = pre / (1.0 + np.exp(-pre)) * f64(gain)[:, None]
    page = f64(page0).copy()
    page[:, unstriped(offs2)] = np.tile(f64(wgs), (H // 128, 1)) * h
    a = page[:, unstriped(offs3)]
    b = page[:, unstriped(offs4)]
    low = np.minimum(a, b)
    page[:, unstriped(offs3)] = low
    page[:, unstriped(offs4)] = a + f64(back)[:, None] * low
    return w4.T @ mxq(page, 0, "e4m3")

@@ -1,0 +1,343 @@
+from contextlib import ExitStack
+
+import concourse.mybir as mybir
+from concourse.masks import make_identity
+
+K, H, N, T, S, T2, PAIRS = 1024, 1024, 512, 4096, 1024, 2048, 512
+FLOPS = 2 * K * H * S + 2 * H * N * T2
+
+F32 = mybir.dt.float32
+BF16 = mybir.dt.bfloat16
+I32 = mybir.dt.int32
+U32 = mybir.dt.uint32
+U16 = mybir.dt.uint16
+U8 = mybir.dt.uint8
+FP8X4 = mybir.dt.float8_e4m3fn_x4
+FP4X4 = mybir.dt.float4_e2m1fn_x4
+ALU = mybir.AluOpType
+ACT = mybir.ActivationFunctionType
+
+P = 128
+PACK = 4
+PASS = P * PACK
+BANK = 512
+PASSES = K // PASS
+ROW_TILES = H // P
+CHUNKS = T2 // BANK
+HALVES = S // BANK
+N_TILES = N // P
+QUADS = 4
+QUAD = P // QUADS
+PAGE_SLOTS = 5
+RELAYS = 3
+ROW_ORDER = [(0, 0), (0, 1), (0, 2), (0, 3), (1, 2), (1, 0), (1, 1), (1, 3)]
+
+
+def tile_list_ramp_merge_forecast_kernel(
+    tc, tab_words, tab_scales, offs, w1, cond, gain, page0, wgs, offs2, offs3, offs4, back, w4_words, w4_scales, out
+):
+    nc = tc.nc
+    with ExitStack() as ctx:
+        held = ctx.enter_context(tc.tile_pool(name="held", bufs=1))
+        shared = ctx.enter_context(tc.tile_pool(name="shared", bufs=1))
+        relay = ctx.enter_context(tc.tile_pool(name="relay", bufs=1))
+        ring2 = ctx.enter_context(tc.tile_pool(name="ring2", bufs=2))
+        ring3 = ctx.enter_context(tc.tile_pool(name="ring3", bufs=3))
+        outs = ctx.enter_context(tc.tile_pool(name="outs", bufs=8))
+        psum = ctx.enter_context(tc.psum_pool(name="psum", bufs=1))
+
+        def bank(index):
+            return psum.tile([P, BANK], F32, name="bank%d" % index)
+
+        def rows_of(matrix, tile_index):
+            b, t = ROW_ORDER[tile_index]
+            return matrix[PASS * b : PASS * (b + 1), :].rearrange("(p t) c -> t p c", t=PACK)[t]
+
+        list1 = held.tile([P, S // 16], U16, name="list1")
+        list2 = held.tile([P, S // 16], U16, name="list2")
+        list3 = held.tile([P, PAIRS // 16], U16, name="list3")
+        list4 = held.tile([P, PAIRS // 16], U16, name="list4")
+        table = [shared.tile([P, T], I32, name="table%d" % a, offset=a * T * 4, align_bytes=64) for a in range(PASSES)]
+        table_scales = held.tile([P, T], U8, name="table_scales", align_bytes=64)
+        nc.vector.memset(table_scales[:].bitcast(I32), 0)
+        nc.sync.dma_start(list1[:], offs)
+        nc.sync.dma_start(table[0][:], tab_words[0].rearrange("p n t -> p (n t)").bitcast(I32))
+        for q in range(QUADS):
+            nc.sync.dma_start(
+                table_scales[QUAD * q : QUAD * q + 4 * PASSES, :].bitcast(I32),
+                tab_scales[:, 4 * q : 4 * q + 4, :].bitcast(I32),
+            )
+        nc.sync.dma_start(table[1][:], tab_words[1].rearrange("p n t -> p (n t)").bitcast(I32))
+
+        def load_w1(a, b):
+            raw = ring2.tile([P, PACK, PASS], F32, name="w1_raw")
+            nc.sync.dma_start(
+                raw[:],
+                w1[PASS * a : PASS * (a + 1), PASS * b : PASS * (b + 1)].rearrange("(p j) c -> p j c", j=PACK),
+            )
+            return raw
+
+        def load_cond(i):
+            tile = ring3.tile([P, S], F32, name="cond_rows")
+            nc.sync.dma_start(tile[:], rows_of(cond, i))
+            return tile
+
+        def load_page(i):
+            tile = held.tile([P, T2], F32, name="page%d" % (i % PAGE_SLOTS))
+            nc.sync.dma_start(tile[:], rows_of(page0, i))
+            return tile
+
+        w1_raw = {(a, 0): load_w1(a, 0) for a in range(PASSES)}
+        conds = {0: load_cond(0)}
+        gains = held.tile([P, H // PASS, PACK], F32, name="gains")
+        backs = held.tile([P, H // PASS, PACK], F32, name="backs")
+        nc.scalar.dma_start(gains[:], gain.rearrange("(b p t) -> p b t", p=P, t=PACK))
+        nc.scalar.dma_start(backs[:], back.rearrange("(b p t) -> p b t", p=P, t=PACK))
+        wgs_rows = wgs.rearrange("(m t) j -> m t j", t=PACK)
+        wgs_first = held.tile([P, S], F32, name="wgs_first")
+        wgs_rest = held.tile([P, PACK - 1, S], F32, name="wgs_rest")
+        for q in range(QUADS):
+            nc.sync.dma_start(wgs_first[QUAD * q : QUAD * (q + 1), :], wgs_rows[:, 0, :])
+        nc.sync.dma_start(list2[:], offs2)
+        pages = {0: load_page(0)}
+        nc.sync.dma_start(list3[:], offs3)
+        nc.sync.dma_start(list4[:], offs4)
+        conds[1] = load_cond(1)
+        for q in range(QUADS):
+            nc.sync.dma_start(wgs_rest[QUAD * q : QUAD * (q + 1), :, :], wgs_rows[:, 1:PACK, :])
+        pages[1] = load_page(1)
+
+        def wgs_of(t):
+            return wgs_first[:] if t == 0 else wgs_rest[:, t - 1, :]
+
+        identity = held.tile([P, P], F32, name="identity")
+        make_identity(nc, identity[:])
+
+        picked = [held.tile([P, S], U32, name="picked%d" % a, align_bytes=64) for a in range(PASSES)]
+        picked_scales = held.tile([P, S], U8, name="picked_scales", align_bytes=64)
+        nc.vector.tensor_copy(picked[0][:], table[0][:].bitcast(U32).indirect(list1[:]))
+        nc.vector.tensor_copy(picked_scales[:], table_scales[:].indirect(list1[:]))
+        nc.vector.tensor_copy(picked[1][:], table[1][:].bitcast(U32).indirect(list1[:]))
+
+        w1_codes = {}
+        w1_scales = {}
+
+        def quantise_w1(a, b, parts):
+            grouped = ring2.tile([P, PACK, P, PACK], BF16, name="w1_grouped", align_bytes=64)
+            codes = held.tile([P, PASS], U32, name="w1_codes%d%d" % (a, b), align_bytes=64)
+            scales = held.tile([P, PASS], U8, name="w1_scales%d%d" % (a, b), align_bytes=64)
+            src = w1_raw[a, b][:].rearrange("p j (m t) -> p m t j", t=PACK)
+            dst = grouped[:].rearrange("p t m j -> p m t j")
+            flat = grouped[:].rearrange("p t m j -> p (t m j)")
+            for t0, t1, cast in parts:
+                cast(dst[:, :, t0:t1, :], src[:, :, t0:t1, :])
+                nc.vector.quantize_mx(
+                    codes[:, P * t0 : P * t1].bitcast(FP8X4), scales[:, P * t0 : P * t1], flat[:, PASS * t0 : PASS * t1]
+                )
+            w1_codes[a, b] = codes
+            w1_scales[a, b] = scales
+
+        for a in range(PASSES):
+            quantise_w1(a, 0, [(0, 1, nc.vector.tensor_copy), (1, PACK, nc.scalar.copy)])
+
+        def first_product(i, half):
+            b, t = ROW_ORDER[i]
+            acc = bank(half)
+            cols = slice(BANK * half, BANK * (half + 1))
+            for a in range(PASSES):
+                nc.tensor.matmul_mx(
+                    acc[:],
+                    lhsT=w1_codes[a, b][:, P * t : P * (t + 1)].bitcast(FP8X4),
+                    lhsT_scale=w1_scales[a, b][:, P * t : P * (t + 1)],
+                    rhs=picked[a][:, cols].bitcast(FP8X4),
+                    rhs_scale=picked_scales[4 * a : P, cols],
+                    start=(a == 0),
+                    stop=(a == PASSES - 1),
+                )
+            return acc
+
+        def relay_tile(name, step, part, width, dtype):
+            offset = ((step % RELAYS) * S + part * PAIRS) * 4
+            return relay.tile([P, width], dtype, name="%s%d" % (name, step), offset=offset, align_bytes=64)
+
+        def states(i, between):
+            b, t = ROW_ORDER[i]
+            h = ring3.tile([P, S], F32, name="h")
+            silu_turned = relay_tile("silu_turned", i - 1, 0, S, F32)
+            for half in range(HALVES):
+                cols = slice(BANK * half, BANK * (half + 1))
+                acc = first_product(i, half)
+                product = ring2.tile([P, BANK], F32, name="product")
+                nc.scalar.copy(product[:], acc[:])
+                turned = bank(HALVES + half)
+                for q in range(BANK // P):
+                    block = slice(P * q, P * (q + 1))
+                    cond_block = slice(BANK * half + P * q, BANK * half + P * (q + 1))
+                    nc.tensor.matmul(
+                        turned[:, block], conds[i][:, cond_block], identity[:], start=True, stop=False, is_transpose=True
+                    )
+                    nc.tensor.matmul(
+                        turned[:, block], product[:, block], identity[:], start=False, stop=True, is_transpose=True
+                    )
+                nc.scalar.activation(silu_turned[:, cols], turned[:], ACT.Silu)
+                upright = bank(2 * HALVES + half)
+                for q in range(BANK // P):
+                    block = slice(P * q, P * (q + 1))
+                    silu_block = slice(BANK * half + P * q, BANK * half + P * (q + 1))
+                    nc.tensor.transpose(upright[:, block], silu_turned[:, silu_block], identity[:])
+                if half == HALVES - 1:
+                    between()
+                nc.scalar.activation(h[:, cols], upright[:], ACT.Copy, scale=gains[:, b, t : t + 1])
+            return h
+
+        def put_first_tile():
+            gained = held.tile([P, S], F32, name="wgs_gained")
+            nc.vector.tensor_scalar(gained[:], wgs_first[:], gains[:, 0, 0:1], None, ALU.mult)
+            silus = []
+            for half in range(HALVES):
+                cols = slice(BANK * half, BANK * (half + 1))
+                acc = first_product(0, half)
+                pre = ring2.tile([P, BANK], F32, name="product")
+                nc.vector.tensor_tensor(pre[:], acc[:], conds[0][:, cols], ALU.add)
+                silu = ring2.tile([P, BANK], F32, name="silu_turned")
+                nc.scalar.activation(silu[:], pre[:], ACT.Silu)
+                silus.append(silu)
+            for half in range(HALVES):
+                cols = slice(BANK * half, BANK * (half + 1))
+                entries = list2[:, BANK // 16 * half : BANK // 16 * (half + 1)]
+                nc.vector.tensor_tensor(pages[0][:].indirect(entries), silus[half][:], gained[:, cols], ALU.mult)
+
+        woven = {}
+        for b in range(H // PASS):
+            for c in range(CHUNKS):
+                woven[b, c] = shared.tile(
+                    [P, BANK, PACK], BF16, name="woven%d%d" % (b, c), offset=(b * CHUNKS + c) * BANK * PACK * 2, align_bytes=64
+                )
+
+        mains, ramps, lows, back_lows = {}, {}, {}, {}
+        last = ROW_TILES - 1
+
+        def fetch(i):
+            mains[i] = relay_tile("main", i, 0, PAIRS, F32)
+            tag = "ramp%d" % i if i in (last - 2, last - 1) else "ramp"
+            ramps[i] = held.tile([P, PAIRS], F32, name=tag, align_bytes=64)
+            nc.vector.tensor_copy(mains[i][:], pages[i][:].indirect(list3[:]))
+            nc.vector.tensor_copy(ramps[i][:], pages[i][:].indirect(list4[:]))
+
+        def minimum(i):
+            lows[i] = held.tile([P, PAIRS], F32, name="low")
+            nc.vector.tensor_tensor(lows[i][:], mains[i][:], ramps[i][:], ALU.min)
+
+        def scale_low(i):
+            b, t = ROW_ORDER[i]
+            back_lows[i] = relay_tile("back_low", i + 1, 1, PAIRS, F32)
+            nc.scalar.activation(back_lows[i][:], lows[i][:], ACT.Copy, scale=backs[:, b, t : t + 1])
+
+        def put_low(i):
+            nc.vector.tensor_copy(pages[i][:].indirect(list3[:]), lows[i][:])
+
+        def put_sum(i):
+            nc.vector.tensor_tensor(pages[i][:].indirect(list4[:]), mains[i][:], back_lows[i][:], ALU.add)
+
+        def round_page(i, c, cast):
+            b, t = ROW_ORDER[i]
+            cast(woven[b, c][:, :, t], pages[i][:, BANK * c : BANK * (c + 1)])
+
+        page_codes = {}
+        page_scales = {}
+
+        def quantise_page(b, c):
+            if b == 0 and c < 2:
+                codes = relay_tile("codes", last - 1 + c, c, BANK, U32)
+            elif b == 0:
+                codes = held.tile([P, BANK], U32, name="ramp%d" % (last - 4 + c), align_bytes=64)
+            else:
+                codes = held.tile([P, BANK], U32, name="page_codes%d" % c, align_bytes=64)
+            scales = held.tile([P, BANK], U8, name="page_scales%d%d" % (b, c), align_bytes=64)
+            nc.vector.quantize_mx(codes[:].bitcast(FP8X4), scales[:], woven[b, c][:].rearrange("p c t -> p (c t)"))
+            page_codes[b, c] = codes
+            page_scales[b, c] = scales
+
+        w4_codes = held.tile([P, H // PASS, 2 * N], U8, name="w4_codes", align_bytes=64)
+        w4_planes = held.tile([P, H // PASS, N], U8, name="w4_planes", align_bytes=64)
+
+        def load_w4():
+            nc.gpsimd.memset(w4_planes[:], 0)
+            nc.sync.dma_start(w4_codes[:].bitcast(I32), w4_words.rearrange("a p c -> p a c").bitcast(I32))
+            for q in range(QUADS):
+                nc.sync.dma_start(
+                    w4_planes[QUAD * q : QUAD * q + 4, :, :].bitcast(I32),
+                    w4_scales[:, 4 * q : 4 * q + 4, :].rearrange("a r n -> r a n").bitcast(I32),
+                )
+
+        scores = {}
+
+        def second_product(b, c, n):
+            if b == 0:
+                scores[c, n] = bank((N_TILES * c + n) % 8)
+            nc.tensor.matmul_mx(
+                scores[c, n][:],
+                lhsT=w4_codes[:, b, 2 * P * n : 2 * P * (n + 1)].bitcast(FP4X4),
+                lhsT_scale=w4_planes[:, b, P * n : P * (n + 1)],
+                rhs=page_codes[b, c][:].bitcast(FP8X4),
+                rhs_scale=page_scales[b, c][:],
+                start=(b == 0),
+                stop=(b == H // PASS - 1),
+            )
+
+        def store(c, n, copy):
+            staged = outs.tile([P, BANK], F32, name="staged")
+            copy(staged[:], scores[c, n][:])
+            nc.sync.dma_start(out[P * n : P * (n + 1), BANK * c : BANK * (c + 1)], staged[:])
+
+        hs = {}
+        put_first_tile()
+        for i in range(ROW_TILES):
+            if i + 2 < ROW_TILES:
+                conds[i + 2] = load_cond(i + 2)
+                pages[i + 2] = load_page(i + 2)
+            if i == 1:
+                for a in range(PASSES):
+                    w1_raw[a, 1] = load_w1(a, 1)
+                    quantise_w1(a, 1, [(0, PACK, nc.scalar.copy)])
+                load_w4()
+            if i == 0:
+                hs[1] = states(1, lambda: None)
+            elif i < last:
+                hs[i + 1] = states(i + 1, lambda: scale_low(i - 1))
+            else:
+                scale_low(i - 1)
+            fetch(i)
+            if i > 0:
+                put_sum(i - 1)
+            minimum(i)
+            if i < last:
+                nc.vector.tensor_tensor(
+                    pages[i + 1][:].indirect(list2[:]), hs[i + 1][:], wgs_of(ROW_ORDER[i + 1][1]), ALU.mult
+                )
+            else:
+                scale_low(i)
+                quantise_page(0, 0)
+            put_low(i)
+            if i > 0:
+                for c in range(CHUNKS):
+                    round_page(i - 1, c, nc.scalar.copy)
+            if i in (last - 2, last - 1):
+                quantise_page(0, i - last + 4)
+        quantise_page(0, 1)
+        put_sum(last)
+        for c in range(2):
+            for n in range(N_TILES):
+                second_product(0, c, n)
+
+        round_page(last, 0, nc.vector.tensor_copy)
+        for c in range(CHUNKS):
+            if c + 1 < CHUNKS:
+                round_page(last, c + 1, nc.vector.tensor_copy)
+            quantise_page(1, c)
+        for c in range(CHUNKS):
+            for n in range(N_TILES):
+                if c >= 2:
+                    second_product(0, c, n)
+                second_product(1, c, n)
+                store(c, n, nc.vector.tensor_copy if c >= 2 and n % 2 == 1 else nc.scalar.copy)

@@ -28,8 +28,9 @@ HALVES = S // BANK
 N_TILES = N // P
 QUADS = 4
 QUAD = P // QUADS
-PAGE_SLOTS = 5
+PAGE_SLOTS = 4
 RELAYS = 3
+W1_LEAD = 2 * P
 ROW_ORDER = [(0, 0), (0, 1), (0, 2), (0, 3), (1, 2), (1, 0), (1, 1), (1, 3)]
 
 
@@ -43,7 +44,7 @@ def tile_list_ramp_merge_forecast_kernel(
         relay = ctx.enter_context(tc.tile_pool(name="relay", bufs=1))
         ring2 = ctx.enter_context(tc.tile_pool(name="ring2", bufs=2))
         ring3 = ctx.enter_context(tc.tile_pool(name="ring3", bufs=3))
-        outs = ctx.enter_context(tc.tile_pool(name="outs", bufs=8))
+        spare = ctx.enter_context(tc.tile_pool(name="spare", bufs=1))
         psum = ctx.enter_context(tc.psum_pool(name="psum", bufs=1))
 
         def bank(index):
@@ -51,6 +52,8 @@ def tile_list_ramp_merge_forecast_kernel(
 
         def rows_of(matrix, tile_index):
             b, t = ROW_ORDER[tile_index]
+            if b == 0:
+                return matrix[P * t : P * (t + 1), :]
             return matrix[PASS * b : PASS * (b + 1), :].rearrange("(p t) c -> t p c", t=PACK)[t]
 
         list1 = held.tile([P, S // 16], U16, name="list1")
@@ -69,16 +72,18 @@ def tile_list_ramp_merge_forecast_kernel(
             )
         nc.sync.dma_start(table[1][:], tab_words[1].rearrange("p n t -> p (n t)").bitcast(I32))
 
-        def load_w1(a, b):
-            raw = ring2.tile([P, PACK, PASS], F32, name="w1_raw")
-            nc.sync.dma_start(
-                raw[:],
-                w1[PASS * a : PASS * (a + 1), PASS * b : PASS * (b + 1)].rearrange("(p j) c -> p j c", j=PACK),
-            )
+        def load_w1(a, c0, c1, tag, offset):
+            raw = spare.tile([P, PACK, c1 - c0], F32, name=tag, offset=offset)
+            nc.sync.dma_start(raw[:], w1[PASS * a : PASS * (a + 1), c0:c1].rearrange("(p j) c -> p j c", j=PACK))
             return raw
 
+        def stage_tile(kind, ring, i):
+            if i >= ROW_TILES - 2:
+                return held.tile([P, S], F32, name="%s%d" % (kind, i), align_bytes=64)
+            return ring.tile([P, S], F32, name=kind)
+
         def load_cond(i):
-            tile = ring3.tile([P, S], F32, name="cond_rows")
+            tile = stage_tile("cond_rows", ring3, i)
             nc.sync.dma_start(tile[:], rows_of(cond, i))
             return tile
 
@@ -87,28 +92,35 @@ def tile_list_ramp_merge_forecast_kernel(
             nc.sync.dma_start(tile[:], rows_of(page0, i))
             return tile
 
-        w1_raw = {(a, 0): load_w1(a, 0) for a in range(PASSES)}
-        conds = {0: load_cond(0)}
-        gains = held.tile([P, H // PASS, PACK], F32, name="gains")
-        backs = held.tile([P, H // PASS, PACK], F32, name="backs")
-        nc.scalar.dma_start(gains[:], gain.rearrange("(b p t) -> p b t", p=P, t=PACK))
-        nc.scalar.dma_start(backs[:], back.rearrange("(b p t) -> p b t", p=P, t=PACK))
-        wgs_rows = wgs.rearrange("(m t) j -> m t j", t=PACK)
-        wgs_first = held.tile([P, S], F32, name="wgs_first")
-        wgs_rest = held.tile([P, PACK - 1, S], F32, name="wgs_rest")
-        for q in range(QUADS):
-            nc.sync.dma_start(wgs_first[QUAD * q : QUAD * (q + 1), :], wgs_rows[:, 0, :])
+        w1_bytes = PACK * PASS * 4
+        w1_first = [load_w1(a, 0, W1_LEAD, "w1_first%d" % a, a * w1_bytes) for a in range(PASSES)]
+        gains = [held.tile([P, PACK], F32, name="gains%d" % b) for b in range(H // PASS)]
+        backs = [held.tile([P, PACK], F32, name="backs%d" % b) for b in range(H // PASS)]
+        with nc.allow_non_contiguous_dma(reason="one value of a channel vector for each partition"):
+            nc.scalar.dma_start(gains[0][:], gain[0:PASS].rearrange("(t p) -> p t", p=P))
+            nc.scalar.dma_start(backs[0][:], back[0:PASS].rearrange("(t p) -> p t", p=P))
+        conds = {0: stage_tile("cond_rows", ring3, 0)}
+        wgs_plain = held.tile([P, S], F32, name="wgs_plain")
+        wgs_dealt = held.tile([P, PACK, S], F32, name="wgs_dealt")
+        nc.sync.dma_start(conds[0][:], rows_of(cond, 0))
+        nc.sync.dma_start(wgs_plain[:], wgs)
         nc.sync.dma_start(list2[:], offs2)
         pages = {0: load_page(0)}
+        conds[1] = load_cond(1)
+        w1_rest = [load_w1(a, W1_LEAD, PASS, "w1_rest%d" % a, a * w1_bytes + PACK * W1_LEAD * 4) for a in range(PASSES)]
         nc.sync.dma_start(list3[:], offs3)
         nc.sync.dma_start(list4[:], offs4)
-        conds[1] = load_cond(1)
-        for q in range(QUADS):
-            nc.sync.dma_start(wgs_rest[QUAD * q : QUAD * (q + 1), :, :], wgs_rows[:, 1:PACK, :])
         pages[1] = load_page(1)
 
-        def wgs_of(t):
-            return wgs_first[:] if t == 0 else wgs_rest[:, t - 1, :]
+        def load_second_pass_constants():
+            nc.sync.dma_start(gains[1][:], gain[PASS:H].rearrange("(p t) -> p t", t=PACK))
+            nc.sync.dma_start(backs[1][:], back[PASS:H].rearrange("(p t) -> p t", t=PACK))
+            for q in range(QUADS):
+                nc.sync.dma_start(wgs_dealt[QUAD * q : QUAD * (q + 1), :, :], wgs.rearrange("(m t) j -> m t j", t=PACK))
+
+        def wgs_of(i):
+            b, t = ROW_ORDER[i]
+            return wgs_plain[:] if b == 0 else wgs_dealt[:, t, :]
 
         identity = held.tile([P, P], F32, name="identity")
         make_identity(nc, identity[:])
@@ -121,24 +133,29 @@ def tile_list_ramp_merge_forecast_kernel(
 
         w1_codes = {}
         w1_scales = {}
+        for a in range(PASSES):
+            for b in range(H // PASS):
+                w1_codes[a, b] = held.tile([P, PASS], U32, name="w1_codes%d%d" % (a, b), align_bytes=64)
+                w1_scales[a, b] = held.tile([P, PASS], U8, name="w1_scales%d%d" % (a, b), align_bytes=64)
 
-        def quantise_w1(a, b, parts):
+        def quantise_w1_plain(a, raw, c0, c1, cast):
+            grouped = ring2.tile([P, c1 - c0, PACK], BF16, name="w1_grouped", align_bytes=64)
+            cast(
+                grouped[:].rearrange("p (c i) j -> p c j i", i=PACK), raw[:].rearrange("p j (c i) -> p c j i", i=PACK)
+            )
+            nc.vector.quantize_mx(
+                w1_codes[a, 0][:, c0:c1].bitcast(FP8X4), w1_scales[a, 0][:, c0:c1], grouped[:].rearrange("p c j -> p (c j)")
+            )
+
+        def quantise_w1_dealt(a, raw):
             grouped = ring2.tile([P, PACK, P, PACK], BF16, name="w1_grouped", align_bytes=64)
-            codes = held.tile([P, PASS], U32, name="w1_codes%d%d" % (a, b), align_bytes=64)
-            scales = held.tile([P, PASS], U8, name="w1_scales%d%d" % (a, b), align_bytes=64)
-            src = w1_raw[a, b][:].rearrange("p j (m t) -> p m t j", t=PACK)
-            dst = grouped[:].rearrange("p t m j -> p m t j")
-            flat = grouped[:].rearrange("p t m j -> p (t m j)")
-            for t0, t1, cast in parts:
-                cast(dst[:, :, t0:t1, :], src[:, :, t0:t1, :])
-                nc.vector.quantize_mx(
-                    codes[:, P * t0 : P * t1].bitcast(FP8X4), scales[:, P * t0 : P * t1], flat[:, PASS * t0 : PASS * t1]
-                )
-            w1_codes[a, b] = codes
-            w1_scales[a, b] = scales
+            nc.scalar.copy(grouped[:].rearrange("p t m j -> p m t j"), raw[:].rearrange("p j (m t) -> p m t j", t=PACK))
+            nc.vector.quantize_mx(
+                w1_codes[a, 1][:].bitcast(FP8X4), w1_scales[a, 1][:], grouped[:].rearrange("p t m j -> p (t m j)")
+            )
 
         for a in range(PASSES):
-            quantise_w1(a, 0, [(0, 1, nc.vector.tensor_copy), (1, PACK, nc.scalar.copy)])
+            quantise_w1_plain(a, w1_first[a], 0, W1_LEAD, nc.vector.tensor_copy)
 
         def first_product(i, half):
             b, t = ROW_ORDER[i]
@@ -164,11 +181,11 @@ def tile_list_ramp_merge_forecast_kernel(
             b, t = ROW_ORDER[i]
             h = ring3.tile([P, S], F32, name="h")
             silu_turned = relay_tile("silu_turned", i - 1, 0, S, F32)
+            product = stage_tile("product", ring2, i)
             for half in range(HALVES):
                 cols = slice(BANK * half, BANK * (half + 1))
                 acc = first_product(i, half)
-                product = ring2.tile([P, BANK], F32, name="product")
-                nc.scalar.copy(product[:], acc[:])
+                nc.scalar.copy(product[:, cols], acc[:])
                 turned = bank(HALVES + half)
                 for q in range(BANK // P):
                     block = slice(P * q, P * (q + 1))
@@ -177,7 +194,7 @@ def tile_list_ramp_merge_forecast_kernel(
                         turned[:, block], conds[i][:, cond_block], identity[:], start=True, stop=False, is_transpose=True
                     )
                     nc.tensor.matmul(
-                        turned[:, block], product[:, block], identity[:], start=False, stop=True, is_transpose=True
+                        turned[:, block], product[:, cond_block], identity[:], start=False, stop=True, is_transpose=True
                     )
                 nc.scalar.activation(silu_turned[:, cols], turned[:], ACT.Silu)
                 upright = bank(2 * HALVES + half)
@@ -187,32 +204,31 @@ def tile_list_ramp_merge_forecast_kernel(
                     nc.tensor.transpose(upright[:, block], silu_turned[:, silu_block], identity[:])
                 if half == HALVES - 1:
                     between()
-                nc.scalar.activation(h[:, cols], upright[:], ACT.Copy, scale=gains[:, b, t : t + 1])
+                nc.scalar.activation(h[:, cols], upright[:], ACT.Copy, scale=gains[b][:, t : t + 1])
             return h
 
         def put_first_tile():
-            gained = held.tile([P, S], F32, name="wgs_gained")
-            nc.vector.tensor_scalar(gained[:], wgs_first[:], gains[:, 0, 0:1], None, ALU.mult)
-            silus = []
+            gained = ring3.tile([P, S], F32, name="h")
+            silu = held.tile([P, S], F32, name="even_planes")
+            nc.vector.tensor_scalar(gained[:], wgs_plain[:], gains[0][:, 0:1], None, ALU.mult)
             for half in range(HALVES):
                 cols = slice(BANK * half, BANK * (half + 1))
                 acc = first_product(0, half)
-                pre = ring2.tile([P, BANK], F32, name="product")
+                pre = ring2.tile([P, BANK], F32, name="rounded")
                 nc.vector.tensor_tensor(pre[:], acc[:], conds[0][:, cols], ALU.add)
-                silu = ring2.tile([P, BANK], F32, name="silu_turned")
-                nc.scalar.activation(silu[:], pre[:], ACT.Silu)
-                silus.append(silu)
+                nc.scalar.activation(silu[:, cols], pre[:], ACT.Silu)
             for half in range(HALVES):
                 cols = slice(BANK * half, BANK * (half + 1))
                 entries = list2[:, BANK // 16 * half : BANK // 16 * (half + 1)]
-                nc.vector.tensor_tensor(pages[0][:].indirect(entries), silus[half][:], gained[:, cols], ALU.mult)
+                nc.vector.tensor_tensor(pages[0][:].indirect(entries), silu[:, cols], gained[:, cols], ALU.mult)
 
         woven = {}
-        for b in range(H // PASS):
-            for c in range(CHUNKS):
-                woven[b, c] = shared.tile(
-                    [P, BANK, PACK], BF16, name="woven%d%d" % (b, c), offset=(b * CHUNKS + c) * BANK * PACK * 2, align_bytes=64
-                )
+        for c in range(CHUNKS):
+            woven[1, c] = shared.tile(
+                [P, BANK, PACK], BF16, name="woven%d" % c, offset=T * 4 + c * BANK * PACK * 2, align_bytes=64
+            )
+        planes = shared.tile([P, PACK, T2], BF16, name="planes", offset=0, align_bytes=64)
+        even_planes = held.tile([P, 2, T2], BF16, name="even_planes")
 
         mains, ramps, lows, back_lows = {}, {}, {}, {}
         last = ROW_TILES - 1
@@ -231,7 +247,7 @@ def tile_list_ramp_merge_forecast_kernel(
         def scale_low(i):
             b, t = ROW_ORDER[i]
             back_lows[i] = relay_tile("back_low", i + 1, 1, PAIRS, F32)
-            nc.scalar.activation(back_lows[i][:], lows[i][:], ACT.Copy, scale=backs[:, b, t : t + 1])
+            nc.scalar.activation(back_lows[i][:], lows[i][:], ACT.Copy, scale=backs[b][:, t : t + 1])
 
         def put_low(i):
             nc.vector.tensor_copy(pages[i][:].indirect(list3[:]), lows[i][:])
@@ -242,6 +258,38 @@ def tile_list_ramp_merge_forecast_kernel(
         def round_page(i, c, cast):
             b, t = ROW_ORDER[i]
             cast(woven[b, c][:, :, t], pages[i][:, BANK * c : BANK * (c + 1)])
+
+        def round_and_deal(i):
+            rounded = ring2.tile([P, T2], BF16, name="rounded")
+            nc.scalar.copy(rounded[:], pages[i][:])
+            for t in range(PACK):
+                nc.sync.dma_start(planes[QUAD * i : QUAD * (i + 1), t, :], rounded[t:P:PACK, :])
+
+        def weave_first_pass(c):
+            tag = "%s%d" % (("cond_rows", "product")[c % 2], last - c // 2)
+            woven[0, c] = held.tile([P, BANK, PACK], BF16, name=tag, align_bytes=64)
+            nc.scalar.copy(
+                woven[0, c][:].rearrange("p (c i) t -> p c t i", i=PACK),
+                planes[:, :, BANK * c : BANK * (c + 1)].rearrange("p t (c i) -> p c t i", i=PACK),
+            )
+
+        def weave_even_planes(c):
+            nc.scalar.copy(
+                woven[1, c][:, :, 0:PACK:2], even_planes[:, :, BANK * c : BANK * (c + 1)].rearrange("p e c -> p c e")
+            )
+
+        def round_finished(i):
+            b, t = ROW_ORDER[i]
+            if b == 0:
+                round_and_deal(i)
+            elif t % 2 == 0:
+                nc.scalar.copy(even_planes[:, t // 2, :], pages[i][:])
+                if t == 0:
+                    for c in range(CHUNKS):
+                        weave_even_planes(c)
+            else:
+                for c in range(CHUNKS):
+                    round_page(i, c, nc.scalar.copy)
 
         page_codes = {}
         page_scales = {}
@@ -286,20 +334,24 @@ def tile_list_ramp_merge_forecast_kernel(
             )
 
         def store(c, n, copy):
-            staged = outs.tile([P, BANK], F32, name="staged")
+            staged = spare.tile(
+                [P, BANK], F32, name="staged%d%d" % (c, n), offset=((N_TILES * c + n) % 8) * BANK * 4
+            )
             copy(staged[:], scores[c, n][:])
             nc.sync.dma_start(out[P * n : P * (n + 1), BANK * c : BANK * (c + 1)], staged[:])
 
         hs = {}
         put_first_tile()
+        for a in range(PASSES):
+            quantise_w1_plain(a, w1_rest[a], W1_LEAD, PASS, nc.scalar.copy)
         for i in range(ROW_TILES):
             if i + 2 < ROW_TILES:
                 conds[i + 2] = load_cond(i + 2)
                 pages[i + 2] = load_page(i + 2)
             if i == 1:
                 for a in range(PASSES):
-                    w1_raw[a, 1] = load_w1(a, 1)
-                    quantise_w1(a, 1, [(0, PACK, nc.scalar.copy)])
+                    quantise_w1_dealt(a, load_w1(a, PASS, H, "w1_dealt%d" % a, a * w1_bytes))
+                load_second_pass_constants()
                 load_w4()
             if i == 0:
                 hs[1] = states(1, lambda: None)
@@ -307,21 +359,23 @@ def tile_list_ramp_merge_forecast_kernel(
                 hs[i + 1] = states(i + 1, lambda: scale_low(i - 1))
             else:
                 scale_low(i - 1)
+            if i in (last - 2, last - 1):
+                for c in range(2):
+                    weave_first_pass(2 * (last - 1 - i) + c)
             fetch(i)
             if i > 0:
                 put_sum(i - 1)
             minimum(i)
             if i < last:
                 nc.vector.tensor_tensor(
-                    pages[i + 1][:].indirect(list2[:]), hs[i + 1][:], wgs_of(ROW_ORDER[i + 1][1]), ALU.mult
+                    pages[i + 1][:].indirect(list2[:]), hs[i + 1][:], wgs_of(i + 1), ALU.mult
                 )
             else:
                 scale_low(i)
                 quantise_page(0, 0)
             put_low(i)
             if i > 0:
-                for c in range(CHUNKS):
-                    round_page(i - 1, c, nc.scalar.copy)
+                round_finished(i - 1)
             if i in (last - 2, last - 1):
                 quantise_page(0, i - last + 4)
         quantise_page(0, 1)
@@ -331,10 +385,13 @@ def tile_list_ramp_merge_forecast_kernel(
                 second_product(0, c, n)
 
         round_page(last, 0, nc.vector.tensor_copy)
-        for c in range(CHUNKS):
-            if c + 1 < CHUNKS:
-                round_page(last, c + 1, nc.vector.tensor_copy)
-            quantise_page(1, c)
+        round_page(last, 1, nc.scalar.copy)
+        quantise_page(1, 0)
+        round_page(last, 2, nc.vector.tensor_copy)
+        quantise_page(1, 1)
+        round_page(last, 3, nc.vector.tensor_copy)
+        quantise_page(1, 2)
+        quantise_page(1, 3)
         for c in range(CHUNKS):
             for n in range(N_TILES):
                 if c >= 2:

@@ -28,7 +28,7 @@ HALVES = S // BANK
 N_TILES = N // P
 QUADS = 4
 QUAD = P // QUADS
-PAGE_SLOTS = 4
+PAGE_SLOTS = 5
 RELAYS = 3
 W1_LEAD = 2 * P
 ROW_ORDER = [(0, 0), (0, 1), (0, 2), (0, 3), (1, 2), (1, 0), (1, 1), (1, 3)]
@@ -48,7 +48,10 @@ def tile_list_ramp_merge_forecast_kernel(
         psum = ctx.enter_context(tc.psum_pool(name="psum", bufs=1))
 
         def bank(index):
-            return psum.tile([P, BANK], F32, name="bank%d" % index)
+            return psum.tile([P, BANK], F32, name="bank%d" % index, offset=index * BANK * 4)
+
+        def bank_pair():
+            return psum.tile([P, S], F32, name="bank_pair", offset=0)
 
         def rows_of(matrix, tile_index):
             b, t = ROW_ORDER[tile_index]
@@ -70,20 +73,24 @@ def tile_list_ramp_merge_forecast_kernel(
                 table_scales[QUAD * q : QUAD * q + 4 * PASSES, :].bitcast(I32),
                 tab_scales[:, 4 * q : 4 * q + 4, :].bitcast(I32),
             )
-        nc.sync.dma_start(table[1][:], tab_words[1].rearrange("p n t -> p (n t)").bitcast(I32))
 
-        def load_w1(a, c0, c1, tag, offset):
-            raw = spare.tile([P, PACK, c1 - c0], F32, name=tag, offset=offset)
+        def load_w1(pool, a, c0, c1, tag, offset):
+            raw = pool.tile([P, PACK, c1 - c0], F32, name=tag, offset=offset)
             nc.sync.dma_start(raw[:], w1[PASS * a : PASS * (a + 1), c0:c1].rearrange("(p j) c -> p j c", j=PACK))
             return raw
 
-        def stage_tile(kind, ring, i):
-            if i >= ROW_TILES - 2:
-                return held.tile([P, S], F32, name="%s%d" % (kind, i), align_bytes=64)
-            return ring.tile([P, S], F32, name=kind)
+        def cond_tile(i):
+            if i in (2, ROW_TILES - 1):
+                return held.tile([P, S], F32, name="cond_rows%d" % i, align_bytes=64)
+            return ring2.tile([P, S], F32, name="cond_rows")
+
+        def product_tag(i):
+            if i == 2:
+                return "product2"
+            return "even_planes" if i == ROW_TILES - 1 else "product_%d" % (i % 2)
 
         def load_cond(i):
-            tile = stage_tile("cond_rows", ring3, i)
+            tile = cond_tile(i)
             nc.sync.dma_start(tile[:], rows_of(cond, i))
             return tile
 
@@ -93,24 +100,31 @@ def tile_list_ramp_merge_forecast_kernel(
             return tile
 
         w1_bytes = PACK * PASS * 4
-        w1_first = [load_w1(a, 0, W1_LEAD, "w1_first%d" % a, a * w1_bytes) for a in range(PASSES)]
+        w1_first = [load_w1(spare, a, 0, W1_LEAD, "w1_first%d" % a, a * w1_bytes) for a in range(PASSES)]
+        nc.sync.dma_start(table[1][:], tab_words[1].rearrange("p n t -> p (n t)").bitcast(I32))
         gains = [held.tile([P, PACK], F32, name="gains%d" % b) for b in range(H // PASS)]
         backs = [held.tile([P, PACK], F32, name="backs%d" % b) for b in range(H // PASS)]
-        with nc.allow_non_contiguous_dma(reason="one value of a channel vector for each partition"):
-            nc.scalar.dma_start(gains[0][:], gain[0:PASS].rearrange("(t p) -> p t", p=P))
-            nc.scalar.dma_start(backs[0][:], back[0:PASS].rearrange("(t p) -> p t", p=P))
-        conds = {0: stage_tile("cond_rows", ring3, 0)}
+        first_gain = held.tile([P, 1], F32, name="first_gain")
+        nc.scalar.dma_start(first_gain[:], gain[0:P].rearrange("(p t) -> p t", t=1))
+        conds = {0: cond_tile(0)}
         wgs_plain = held.tile([P, S], F32, name="wgs_plain")
         wgs_dealt = held.tile([P, PACK, S], F32, name="wgs_dealt")
         nc.sync.dma_start(conds[0][:], rows_of(cond, 0))
-        nc.sync.dma_start(wgs_plain[:], wgs)
+        nc.sync.dma_start(wgs_plain[:, 0:BANK], wgs[:, 0:BANK])
         nc.sync.dma_start(list2[:], offs2)
         pages = {0: load_page(0)}
+        nc.sync.dma_start(wgs_plain[:, BANK:S], wgs[:, BANK:S])
         conds[1] = load_cond(1)
-        w1_rest = [load_w1(a, W1_LEAD, PASS, "w1_rest%d" % a, a * w1_bytes + PACK * W1_LEAD * 4) for a in range(PASSES)]
+        with nc.allow_non_contiguous_dma(reason="one value of a channel vector for each partition"):
+            nc.sync.dma_start(gains[0][:, 1:PACK], gain[P:PASS].rearrange("(t p) -> p t", p=P))
+        w1_rest = [load_w1(spare, a, W1_LEAD, PASS, "w1_rest%d" % a, a * w1_bytes + PACK * W1_LEAD * 4) for a in range(PASSES)]
         nc.sync.dma_start(list3[:], offs3)
         nc.sync.dma_start(list4[:], offs4)
         pages[1] = load_page(1)
+        with nc.allow_non_contiguous_dma(reason="one value of a channel vector for each partition"):
+            nc.sync.dma_start(backs[0][:], back[0:PASS].rearrange("(t p) -> p t", p=P))
+        conds[2] = load_cond(2)
+        w1_dealt = [load_w1(shared, a, PASS, H, "w1_dealt%d" % a, T * 4 + a * w1_bytes) for a in range(PASSES)]
 
         def load_second_pass_constants():
             nc.sync.dma_start(gains[1][:], gain[PASS:H].rearrange("(p t) -> p t", t=PACK))
@@ -129,7 +143,6 @@ def tile_list_ramp_merge_forecast_kernel(
         picked_scales = held.tile([P, S], U8, name="picked_scales", align_bytes=64)
         nc.vector.tensor_copy(picked[0][:], table[0][:].bitcast(U32).indirect(list1[:]))
         nc.vector.tensor_copy(picked_scales[:], table_scales[:].indirect(list1[:]))
-        nc.vector.tensor_copy(picked[1][:], table[1][:].bitcast(U32).indirect(list1[:]))
 
         w1_codes = {}
         w1_scales = {}
@@ -148,7 +161,7 @@ def tile_list_ramp_merge_forecast_kernel(
             )
 
         def quantise_w1_dealt(a, raw):
-            grouped = ring2.tile([P, PACK, P, PACK], BF16, name="w1_grouped", align_bytes=64)
+            grouped = held.tile([P, PACK, P, PACK], BF16, name="%s2" % ("cond_rows", "product")[a], align_bytes=64)
             nc.scalar.copy(grouped[:].rearrange("p t m j -> p m t j"), raw[:].rearrange("p j (m t) -> p m t j", t=PACK))
             nc.vector.quantize_mx(
                 w1_codes[a, 1][:].bitcast(FP8X4), w1_scales[a, 1][:], grouped[:].rearrange("p t m j -> p (t m j)")
@@ -156,14 +169,18 @@ def tile_list_ramp_merge_forecast_kernel(
 
         for a in range(PASSES):
             quantise_w1_plain(a, w1_first[a], 0, W1_LEAD, nc.vector.tensor_copy)
+        for half in range(HALVES):
+            nc.vector.tensor_copy(
+                picked[1][:, BANK * half : BANK * (half + 1)],
+                table[1][:].bitcast(U32).indirect(list1[:, BANK // 16 * half : BANK // 16 * (half + 1)]),
+            )
 
-        def first_product(i, half):
+        def first_product(i, half, acc):
             b, t = ROW_ORDER[i]
-            acc = bank(half)
             cols = slice(BANK * half, BANK * (half + 1))
             for a in range(PASSES):
                 nc.tensor.matmul_mx(
-                    acc[:],
+                    acc[:, cols],
                     lhsT=w1_codes[a, b][:, P * t : P * (t + 1)].bitcast(FP8X4),
                     lhsT_scale=w1_scales[a, b][:, P * t : P * (t + 1)],
                     rhs=picked[a][:, cols].bitcast(FP8X4),
@@ -171,7 +188,6 @@ def tile_list_ramp_merge_forecast_kernel(
                     start=(a == 0),
                     stop=(a == PASSES - 1),
                 )
-            return acc
 
         def relay_tile(name, step, part, width, dtype):
             offset = ((step % RELAYS) * S + part * PAIRS) * 4
@@ -181,42 +197,48 @@ def tile_list_ramp_merge_forecast_kernel(
             b, t = ROW_ORDER[i]
             h = ring3.tile([P, S], F32, name="h")
             silu_turned = relay_tile("silu_turned", i - 1, 0, S, F32)
-            product = stage_tile("product", ring2, i)
+            product = held.tile([P, S], F32, name=product_tag(i), align_bytes=64)
+            acc = bank_pair()
             for half in range(HALVES):
                 cols = slice(BANK * half, BANK * (half + 1))
-                acc = first_product(i, half)
-                nc.scalar.copy(product[:, cols], acc[:])
+                first_product(i, half, acc)
+                nc.scalar.copy(product[:, cols], acc[:, cols])
+            for half in range(HALVES):
+                cols = slice(BANK * half, BANK * (half + 1))
                 turned = bank(HALVES + half)
                 for q in range(BANK // P):
                     block = slice(P * q, P * (q + 1))
-                    cond_block = slice(BANK * half + P * q, BANK * half + P * (q + 1))
+                    source = slice(BANK * half + P * q, BANK * half + P * (q + 1))
                     nc.tensor.matmul(
-                        turned[:, block], conds[i][:, cond_block], identity[:], start=True, stop=False, is_transpose=True
+                        turned[:, block], conds[i][:, source], identity[:], start=True, stop=False, is_transpose=True
                     )
                     nc.tensor.matmul(
-                        turned[:, block], product[:, cond_block], identity[:], start=False, stop=True, is_transpose=True
+                        turned[:, block], product[:, source], identity[:], start=False, stop=True, is_transpose=True
                     )
                 nc.scalar.activation(silu_turned[:, cols], turned[:], ACT.Silu)
-                upright = bank(2 * HALVES + half)
+            upright = bank_pair()
+            for half in range(HALVES):
+                cols = slice(BANK * half, BANK * (half + 1))
                 for q in range(BANK // P):
-                    block = slice(P * q, P * (q + 1))
-                    silu_block = slice(BANK * half + P * q, BANK * half + P * (q + 1))
-                    nc.tensor.transpose(upright[:, block], silu_turned[:, silu_block], identity[:])
+                    block = slice(BANK * half + P * q, BANK * half + P * (q + 1))
+                    nc.tensor.transpose(upright[:, block], silu_turned[:, block], identity[:])
                 if half == HALVES - 1:
                     between()
-                nc.scalar.activation(h[:, cols], upright[:], ACT.Copy, scale=gains[b][:, t : t + 1])
+                nc.scalar.activation(h[:, cols], upright[:, cols], ACT.Copy, scale=gains[b][:, t : t + 1])
             return h
 
         def put_first_tile():
             gained = ring3.tile([P, S], F32, name="h")
-            silu = held.tile([P, S], F32, name="even_planes")
-            nc.vector.tensor_scalar(gained[:], wgs_plain[:], gains[0][:, 0:1], None, ALU.mult)
+            silu = held.tile([P, S], F32, name="even_planes", align_bytes=64)
+            acc = bank_pair()
+            pre = held.tile([P, S], F32, name=product_tag(0), align_bytes=64)
+            nc.vector.tensor_scalar(gained[:, 0:BANK], wgs_plain[:, 0:BANK], first_gain[:], None, ALU.mult)
             for half in range(HALVES):
                 cols = slice(BANK * half, BANK * (half + 1))
-                acc = first_product(0, half)
-                pre = ring2.tile([P, BANK], F32, name="rounded")
-                nc.vector.tensor_tensor(pre[:], acc[:], conds[0][:, cols], ALU.add)
-                nc.scalar.activation(silu[:, cols], pre[:], ACT.Silu)
+                first_product(0, half, acc)
+                nc.vector.tensor_tensor(pre[:, cols], acc[:, cols], conds[0][:, cols], ALU.add)
+                nc.scalar.activation(silu[:, cols], pre[:, cols], ACT.Silu)
+            nc.scalar.activation(gained[:, BANK:S], wgs_plain[:, BANK:S], ACT.Copy, scale=first_gain[:])
             for half in range(HALVES):
                 cols = slice(BANK * half, BANK * (half + 1))
                 entries = list2[:, BANK // 16 * half : BANK // 16 * (half + 1)]
@@ -228,7 +250,7 @@ def tile_list_ramp_merge_forecast_kernel(
                 [P, BANK, PACK], BF16, name="woven%d" % c, offset=T * 4 + c * BANK * PACK * 2, align_bytes=64
             )
         planes = shared.tile([P, PACK, T2], BF16, name="planes", offset=0, align_bytes=64)
-        even_planes = held.tile([P, 2, T2], BF16, name="even_planes")
+        even_planes = held.tile([P, 2, T2], BF16, name="even_planes", align_bytes=64)
 
         mains, ramps, lows, back_lows = {}, {}, {}, {}
         last = ROW_TILES - 1
@@ -260,14 +282,18 @@ def tile_list_ramp_merge_forecast_kernel(
             cast(woven[b, c][:, :, t], pages[i][:, BANK * c : BANK * (c + 1)])
 
         def round_and_deal(i):
-            rounded = ring2.tile([P, T2], BF16, name="rounded")
+            rounded = held.tile([P, T2], BF16, name=product_tag(i + 3), align_bytes=64)
             nc.scalar.copy(rounded[:], pages[i][:])
             for t in range(PACK):
                 nc.sync.dma_start(planes[QUAD * i : QUAD * (i + 1), t, :], rounded[t:P:PACK, :])
 
         def weave_first_pass(c):
-            tag = "%s%d" % (("cond_rows", "product")[c % 2], last - c // 2)
-            woven[0, c] = held.tile([P, BANK, PACK], BF16, name=tag, align_bytes=64)
+            if c == 0:
+                woven[0, c] = held.tile([P, BANK, PACK], BF16, name="cond_rows%d" % last, align_bytes=64)
+            else:
+                woven[0, c] = spare.tile(
+                    [P, BANK, PACK], BF16, name="woven_first%d" % c, offset=c * BANK * PACK * 2, align_bytes=64
+                )
             nc.scalar.copy(
                 woven[0, c][:].rearrange("p (c i) t -> p c t i", i=PACK),
                 planes[:, :, BANK * c : BANK * (c + 1)].rearrange("p t (c i) -> p c t i", i=PACK),
@@ -334,7 +360,7 @@ def tile_list_ramp_merge_forecast_kernel(
             )
 
         def store(c, n, copy):
-            staged = spare.tile(
+            staged = (spare if c < 2 else shared).tile(
                 [P, BANK], F32, name="staged%d%d" % (c, n), offset=((N_TILES * c + n) % 8) * BANK * 4
             )
             copy(staged[:], scores[c, n][:])
@@ -342,26 +368,32 @@ def tile_list_ramp_merge_forecast_kernel(
 
         hs = {}
         put_first_tile()
-        for a in range(PASSES):
-            quantise_w1_plain(a, w1_rest[a], W1_LEAD, PASS, nc.scalar.copy)
         for i in range(ROW_TILES):
             if i + 2 < ROW_TILES:
-                conds[i + 2] = load_cond(i + 2)
                 pages[i + 2] = load_page(i + 2)
+            if i + 3 < ROW_TILES:
+                conds[i + 3] = load_cond(i + 3)
             if i == 1:
-                for a in range(PASSES):
-                    quantise_w1_dealt(a, load_w1(a, PASS, H, "w1_dealt%d" % a, a * w1_bytes))
                 load_second_pass_constants()
                 load_w4()
             if i == 0:
                 hs[1] = states(1, lambda: None)
+                for a in range(PASSES):
+                    quantise_w1_plain(a, w1_rest[a], W1_LEAD, PASS, nc.scalar.copy)
             elif i < last:
                 hs[i + 1] = states(i + 1, lambda: scale_low(i - 1))
+                if i == 1:
+                    for a in range(PASSES):
+                        quantise_w1_dealt(a, w1_dealt[a])
             else:
                 scale_low(i - 1)
-            if i in (last - 2, last - 1):
-                for c in range(2):
-                    weave_first_pass(2 * (last - 1 - i) + c)
+            if 2 <= i < last:
+                round_finished(i - 2)
+            if i == last - 2:
+                for c in (2, 3, 1):
+                    weave_first_pass(c)
+            if i == last - 1:
+                weave_first_pass(0)
             fetch(i)
             if i > 0:
                 put_sum(i - 1)
@@ -374,7 +406,7 @@ def tile_list_ramp_merge_forecast_kernel(
                 scale_low(i)
                 quantise_page(0, 0)
             put_low(i)
-            if i > 0:
+            if i >= last - 1:
                 round_finished(i - 1)
             if i in (last - 2, last - 1):
                 quantise_page(0, i - last + 4)
@@ -385,11 +417,11 @@ def tile_list_ramp_merge_forecast_kernel(
                 second_product(0, c, n)
 
         round_page(last, 0, nc.vector.tensor_copy)
-        round_page(last, 1, nc.scalar.copy)
+        round_page(last, 1, nc.vector.tensor_copy)
+        round_page(last, 3, nc.scalar.copy)
         quantise_page(1, 0)
         round_page(last, 2, nc.vector.tensor_copy)
         quantise_page(1, 1)
-        round_page(last, 3, nc.vector.tensor_copy)
         quantise_page(1, 2)
         quantise_page(1, 3)
         for c in range(CHUNKS):

@@ -21,17 +21,24 @@ P = 128
 PACK = 4
 PASS = P * PACK
 BANK = 512
-PASSES = K // PASS
+BANKS = 8
+K_PASSES = K // PASS
+R_PASSES = H // PASS
 ROW_TILES = H // P
+LAST = ROW_TILES - 1
 CHUNKS = T2 // BANK
+HELD_CHUNKS = BANKS * P // N
 HALVES = S // BANK
 N_TILES = N // P
 QUADS = 4
 QUAD = P // QUADS
+SCALE_ROWS = 4
+LIST_ROWS = 16
 PAGE_SLOTS = 5
 RELAYS = 3
-W1_LEAD = 2 * P
-ROW_ORDER = [(0, 0), (0, 1), (0, 2), (0, 3), (1, 2), (1, 0), (1, 1), (1, 3)]
+ROUND_LAG = 3
+W1_DEALT_AFTER = 2
+ROW_ORDER = [(0, t) for t in range(PACK)] + [(1, t) for t in (2, 0, 1, 3)]
 
 
 def tile_list_ramp_merge_forecast_kernel(
@@ -53,44 +60,51 @@ def tile_list_ramp_merge_forecast_kernel(
         def bank_pair():
             return psum.tile([P, S], F32, name="bank_pair", offset=0)
 
-        def rows_of(matrix, tile_index):
-            b, t = ROW_ORDER[tile_index]
+        def rows_of(matrix, i):
+            b, t = ROW_ORDER[i]
             if b == 0:
                 return matrix[P * t : P * (t + 1), :]
             return matrix[PASS * b : PASS * (b + 1), :].rearrange("(p t) c -> t p c", t=PACK)[t]
 
-        list1 = held.tile([P, S // 16], U16, name="list1")
-        list2 = held.tile([P, S // 16], U16, name="list2")
-        list3 = held.tile([P, PAIRS // 16], U16, name="list3")
-        list4 = held.tile([P, PAIRS // 16], U16, name="list4")
-        table = [shared.tile([P, T], I32, name="table%d" % a, offset=a * T * 4, align_bytes=64) for a in range(PASSES)]
+        def list_half(entries, half):
+            return entries[:, BANK // LIST_ROWS * half : BANK // LIST_ROWS * (half + 1)]
+
+        list1 = held.tile([P, S // LIST_ROWS], U16, name="list1")
+        list2 = held.tile([P, S // LIST_ROWS], U16, name="list2")
+        list3 = held.tile([P, PAIRS // LIST_ROWS], U16, name="list3")
+        list4 = held.tile([P, PAIRS // LIST_ROWS], U16, name="list4")
+        table = [shared.tile([P, T], I32, name="table%d" % a, offset=a * T * 4, align_bytes=64) for a in range(K_PASSES)]
         table_scales = held.tile([P, T], U8, name="table_scales", align_bytes=64)
         nc.vector.memset(table_scales[:].bitcast(I32), 0)
         nc.sync.dma_start(list1[:], offs)
         nc.sync.dma_start(table[0][:], tab_words[0].rearrange("p n t -> p (n t)").bitcast(I32))
         for q in range(QUADS):
-            nc.sync.dma_start(
-                table_scales[QUAD * q : QUAD * q + 4 * PASSES, :].bitcast(I32),
-                tab_scales[:, 4 * q : 4 * q + 4, :].bitcast(I32),
+            nc.gpsimd.dma_start(
+                table_scales[QUAD * q : QUAD * q + SCALE_ROWS * K_PASSES, :].bitcast(I32),
+                tab_scales[:, SCALE_ROWS * q : SCALE_ROWS * (q + 1), :].bitcast(I32),
             )
 
-        def load_w1(pool, a, c0, c1, tag, offset):
-            raw = pool.tile([P, PACK, c1 - c0], F32, name=tag, offset=offset)
-            nc.sync.dma_start(raw[:], w1[PASS * a : PASS * (a + 1), c0:c1].rearrange("(p j) c -> p j c", j=PACK))
-            return raw
-
-        def cond_tile(i):
-            if i in (2, ROW_TILES - 1):
-                return held.tile([P, S], F32, name="cond_rows%d" % i, align_bytes=64)
-            return ring2.tile([P, S], F32, name="cond_rows")
+        def load_w1(pool, start, c0, c1):
+            tiles = []
+            for a in range(K_PASSES):
+                offset = start + (a * PASS + c0 % PASS) * PACK * 4
+                raw = pool.tile([P, PACK, c1 - c0], F32, name="w1_raw%d_%d" % (a, c0), offset=offset)
+                nc.sync.dma_start(raw[:], w1[PASS * a : PASS * (a + 1), c0:c1].rearrange("(p j) c -> p j c", j=PACK))
+                tiles.append(raw)
+            return tiles
 
         def product_tag(i):
-            if i == 2:
-                return "product2"
-            return "even_planes" if i == ROW_TILES - 1 else "product_%d" % (i % 2)
+            if i == W1_DEALT_AFTER:
+                return "product_then_w1"
+            return "even_planes" if i == LAST else "product_%d" % (i % 2)
 
         def load_cond(i):
-            tile = cond_tile(i)
+            if i == W1_DEALT_AFTER:
+                tile = held.tile([P, S], F32, name="cond_then_w1", align_bytes=64)
+            elif i == LAST:
+                tile = held.tile([P, S], F32, name="cond_then_woven", align_bytes=64)
+            else:
+                tile = ring2.tile([P, S], F32, name="cond_rows")
             nc.sync.dma_start(tile[:], rows_of(cond, i))
             return tile
 
@@ -99,32 +113,31 @@ def tile_list_ramp_merge_forecast_kernel(
             nc.sync.dma_start(tile[:], rows_of(page0, i))
             return tile
 
-        w1_bytes = PACK * PASS * 4
-        w1_first = [load_w1(spare, a, 0, W1_LEAD, "w1_first%d" % a, a * w1_bytes) for a in range(PASSES)]
+        w1_tile0 = load_w1(spare, 0, 0, P)
         nc.sync.dma_start(table[1][:], tab_words[1].rearrange("p n t -> p (n t)").bitcast(I32))
-        gains = [held.tile([P, PACK], F32, name="gains%d" % b) for b in range(H // PASS)]
-        backs = [held.tile([P, PACK], F32, name="backs%d" % b) for b in range(H // PASS)]
+        gains = [held.tile([P, PACK], F32, name="gains%d" % b) for b in range(R_PASSES)]
+        backs = [held.tile([P, PACK], F32, name="backs%d" % b) for b in range(R_PASSES)]
         first_gain = held.tile([P, 1], F32, name="first_gain")
         nc.scalar.dma_start(first_gain[:], gain[0:P].rearrange("(p t) -> p t", t=1))
-        conds = {0: cond_tile(0)}
         wgs_plain = held.tile([P, S], F32, name="wgs_plain")
         wgs_dealt = held.tile([P, PACK, S], F32, name="wgs_dealt")
-        nc.sync.dma_start(conds[0][:], rows_of(cond, 0))
+        conds = {0: load_cond(0)}
         nc.sync.dma_start(wgs_plain[:, 0:BANK], wgs[:, 0:BANK])
         nc.sync.dma_start(list2[:], offs2)
         pages = {0: load_page(0)}
+        w1_tile1 = load_w1(spare, 0, P, 2 * P)
         nc.sync.dma_start(wgs_plain[:, BANK:S], wgs[:, BANK:S])
         conds[1] = load_cond(1)
         with nc.allow_non_contiguous_dma(reason="one value of a channel vector for each partition"):
             nc.sync.dma_start(gains[0][:, 1:PACK], gain[P:PASS].rearrange("(t p) -> p t", p=P))
-        w1_rest = [load_w1(spare, a, W1_LEAD, PASS, "w1_rest%d" % a, a * w1_bytes + PACK * W1_LEAD * 4) for a in range(PASSES)]
+        w1_rest = load_w1(spare, 0, 2 * P, PASS)
         nc.sync.dma_start(list3[:], offs3)
         nc.sync.dma_start(list4[:], offs4)
         pages[1] = load_page(1)
         with nc.allow_non_contiguous_dma(reason="one value of a channel vector for each partition"):
             nc.sync.dma_start(backs[0][:], back[0:PASS].rearrange("(t p) -> p t", p=P))
         conds[2] = load_cond(2)
-        w1_dealt = [load_w1(shared, a, PASS, H, "w1_dealt%d" % a, T * 4 + a * w1_bytes) for a in range(PASSES)]
+        w1_upper = load_w1(shared, T * 4, PASS, H)
 
         def load_second_pass_constants():
             nc.sync.dma_start(gains[1][:], gain[PASS:H].rearrange("(p t) -> p t", t=PACK))
@@ -139,64 +152,71 @@ def tile_list_ramp_merge_forecast_kernel(
         identity = held.tile([P, P], F32, name="identity")
         make_identity(nc, identity[:])
 
-        picked = [held.tile([P, S], U32, name="picked%d" % a, align_bytes=64) for a in range(PASSES)]
+        picked = [held.tile([P, S], U32, name="picked%d" % a, align_bytes=64) for a in range(K_PASSES)]
         picked_scales = held.tile([P, S], U8, name="picked_scales", align_bytes=64)
         nc.vector.tensor_copy(picked[0][:], table[0][:].bitcast(U32).indirect(list1[:]))
         nc.vector.tensor_copy(picked_scales[:], table_scales[:].indirect(list1[:]))
 
         w1_codes = {}
         w1_scales = {}
-        for a in range(PASSES):
-            for b in range(H // PASS):
+        for a in range(K_PASSES):
+            for b in range(R_PASSES):
                 w1_codes[a, b] = held.tile([P, PASS], U32, name="w1_codes%d%d" % (a, b), align_bytes=64)
                 w1_scales[a, b] = held.tile([P, PASS], U8, name="w1_scales%d%d" % (a, b), align_bytes=64)
 
-        def quantise_w1_plain(a, raw, c0, c1, cast):
-            grouped = ring2.tile([P, c1 - c0, PACK], BF16, name="w1_grouped", align_bytes=64)
-            cast(
-                grouped[:].rearrange("p (c i) j -> p c j i", i=PACK), raw[:].rearrange("p j (c i) -> p c j i", i=PACK)
-            )
-            nc.vector.quantize_mx(
-                w1_codes[a, 0][:, c0:c1].bitcast(FP8X4), w1_scales[a, 0][:, c0:c1], grouped[:].rearrange("p c j -> p (c j)")
-            )
+        def quantise_w1_plain(raws, c0, c1, cast):
+            for a, raw in enumerate(raws):
+                w1_woven = ring2.tile([P, c1 - c0, PACK], BF16, name="w1_woven", align_bytes=64)
+                cast(
+                    w1_woven[:].rearrange("p (c e) j -> p c j e", e=PACK),
+                    raw[:].rearrange("p j (c e) -> p c j e", e=PACK),
+                )
+                nc.vector.quantize_mx(
+                    w1_codes[a, 0][:, c0:c1].bitcast(FP8X4),
+                    w1_scales[a, 0][:, c0:c1],
+                    w1_woven[:].rearrange("p c j -> p (c j)"),
+                )
 
-        def quantise_w1_dealt(a, raw):
-            grouped = held.tile([P, PACK, P, PACK], BF16, name="%s2" % ("cond_rows", "product")[a], align_bytes=64)
-            nc.scalar.copy(grouped[:].rearrange("p t m j -> p m t j"), raw[:].rearrange("p j (m t) -> p m t j", t=PACK))
-            nc.vector.quantize_mx(
-                w1_codes[a, 1][:].bitcast(FP8X4), w1_scales[a, 1][:], grouped[:].rearrange("p t m j -> p (t m j)")
-            )
+        def quantise_w1_dealt(raws):
+            for a, raw in enumerate(raws):
+                tag = ("cond_then_w1", "product_then_w1")[a]
+                w1_woven = held.tile([P, PACK, P, PACK], BF16, name=tag, align_bytes=64)
+                nc.scalar.copy(
+                    w1_woven[:].rearrange("p t m j -> p m t j"), raw[:].rearrange("p j (m t) -> p m t j", t=PACK)
+                )
+                nc.vector.quantize_mx(
+                    w1_codes[a, 1][:].bitcast(FP8X4), w1_scales[a, 1][:], w1_woven[:].rearrange("p t m j -> p (t m j)")
+                )
 
-        for a in range(PASSES):
-            quantise_w1_plain(a, w1_first[a], 0, W1_LEAD, nc.vector.tensor_copy)
+        quantise_w1_plain(w1_tile0, 0, P, nc.vector.tensor_copy)
         for half in range(HALVES):
             nc.vector.tensor_copy(
                 picked[1][:, BANK * half : BANK * (half + 1)],
-                table[1][:].bitcast(U32).indirect(list1[:, BANK // 16 * half : BANK // 16 * (half + 1)]),
+                table[1][:].bitcast(U32).indirect(list_half(list1, half)),
             )
 
         def first_product(i, half, acc):
             b, t = ROW_ORDER[i]
             cols = slice(BANK * half, BANK * (half + 1))
-            for a in range(PASSES):
+            for a in range(K_PASSES):
                 nc.tensor.matmul_mx(
                     acc[:, cols],
                     lhsT=w1_codes[a, b][:, P * t : P * (t + 1)].bitcast(FP8X4),
                     lhsT_scale=w1_scales[a, b][:, P * t : P * (t + 1)],
                     rhs=picked[a][:, cols].bitcast(FP8X4),
-                    rhs_scale=picked_scales[4 * a : P, cols],
+                    rhs_scale=picked_scales[SCALE_ROWS * a : P, cols],
                     start=(a == 0),
-                    stop=(a == PASSES - 1),
+                    stop=(a == K_PASSES - 1),
                 )
 
         def relay_tile(name, step, part, width, dtype):
             offset = ((step % RELAYS) * S + part * PAIRS) * 4
-            return relay.tile([P, width], dtype, name="%s%d" % (name, step), offset=offset, align_bytes=64)
+            return relay.tile([P, width], dtype, name=name, offset=offset, align_bytes=64)
 
         def states(i, between):
             b, t = ROW_ORDER[i]
             h = ring3.tile([P, S], F32, name="h")
-            silu_turned = relay_tile("silu_turned", i - 1, 0, S, F32)
+            silu_turned = relay_tile("silu_turned%d" % i, i - 1, 0, S, F32)
             product = held.tile([P, S], F32, name=product_tag(i), align_bytes=64)
             acc = bank_pair()
             for half in range(HALVES):
@@ -241,8 +261,8 @@ def tile_list_ramp_merge_forecast_kernel(
             nc.scalar.activation(gained[:, BANK:S], wgs_plain[:, BANK:S], ACT.Copy, scale=first_gain[:])
             for half in range(HALVES):
                 cols = slice(BANK * half, BANK * (half + 1))
-                entries = list2[:, BANK // 16 * half : BANK // 16 * (half + 1)]
-                nc.vector.tensor_tensor(pages[0][:].indirect(entries), silu[:, cols], gained[:, cols], ALU.mult)
+                window = pages[0][:].indirect(list_half(list2, half))
+                nc.vector.tensor_tensor(window, silu[:, cols], gained[:, cols], ALU.mult)
 
         woven = {}
         for c in range(CHUNKS):
@@ -253,11 +273,10 @@ def tile_list_ramp_merge_forecast_kernel(
         even_planes = held.tile([P, 2, T2], BF16, name="even_planes", align_bytes=64)
 
         mains, ramps, lows, back_lows = {}, {}, {}, {}
-        last = ROW_TILES - 1
 
         def fetch(i):
-            mains[i] = relay_tile("main", i, 0, PAIRS, F32)
-            tag = "ramp%d" % i if i in (last - 2, last - 1) else "ramp"
+            mains[i] = relay_tile("main%d" % i, i if i > 0 else -1, 0, PAIRS, F32)
+            tag = "ramp_then_codes%d" % i if i in (LAST - 2, LAST - 1) else "ramp"
             ramps[i] = held.tile([P, PAIRS], F32, name=tag, align_bytes=64)
             nc.vector.tensor_copy(mains[i][:], pages[i][:].indirect(list3[:]))
             nc.vector.tensor_copy(ramps[i][:], pages[i][:].indirect(list4[:]))
@@ -268,8 +287,11 @@ def tile_list_ramp_merge_forecast_kernel(
 
         def scale_low(i):
             b, t = ROW_ORDER[i]
-            back_lows[i] = relay_tile("back_low", i + 1, 1, PAIRS, F32)
+            back_lows[i] = relay_tile("back_low%d" % i, i + 1, 1, PAIRS, F32)
             nc.scalar.activation(back_lows[i][:], lows[i][:], ACT.Copy, scale=backs[b][:, t : t + 1])
+
+        def put_states(i, h):
+            nc.vector.tensor_tensor(pages[i][:].indirect(list2[:]), h[:], wgs_of(i), ALU.mult)
 
         def put_low(i):
             nc.vector.tensor_copy(pages[i][:].indirect(list3[:]), lows[i][:])
@@ -277,26 +299,26 @@ def tile_list_ramp_merge_forecast_kernel(
         def put_sum(i):
             nc.vector.tensor_tensor(pages[i][:].indirect(list4[:]), mains[i][:], back_lows[i][:], ALU.add)
 
-        def round_page(i, c, cast):
+        def round_into_woven(i, c, cast):
             b, t = ROW_ORDER[i]
             cast(woven[b, c][:, :, t], pages[i][:, BANK * c : BANK * (c + 1)])
 
         def round_and_deal(i):
-            rounded = held.tile([P, T2], BF16, name=product_tag(i + 3), align_bytes=64)
+            rounded = held.tile([P, T2], BF16, name=product_tag(i + ROUND_LAG), align_bytes=64)
             nc.scalar.copy(rounded[:], pages[i][:])
             for t in range(PACK):
                 nc.sync.dma_start(planes[QUAD * i : QUAD * (i + 1), t, :], rounded[t:P:PACK, :])
 
         def weave_first_pass(c):
             if c == 0:
-                woven[0, c] = held.tile([P, BANK, PACK], BF16, name="cond_rows%d" % last, align_bytes=64)
+                woven[0, c] = held.tile([P, BANK, PACK], BF16, name="cond_then_woven", align_bytes=64)
             else:
                 woven[0, c] = spare.tile(
                     [P, BANK, PACK], BF16, name="woven_first%d" % c, offset=c * BANK * PACK * 2, align_bytes=64
                 )
             nc.scalar.copy(
-                woven[0, c][:].rearrange("p (c i) t -> p c t i", i=PACK),
-                planes[:, :, BANK * c : BANK * (c + 1)].rearrange("p t (c i) -> p c t i", i=PACK),
+                woven[0, c][:].rearrange("p (c e) t -> p c t e", e=PACK),
+                planes[:, :, BANK * c : BANK * (c + 1)].rearrange("p t (c e) -> p c t e", e=PACK),
             )
 
         def weave_even_planes(c):
@@ -315,16 +337,16 @@ def tile_list_ramp_merge_forecast_kernel(
                         weave_even_planes(c)
             else:
                 for c in range(CHUNKS):
-                    round_page(i, c, nc.scalar.copy)
+                    round_into_woven(i, c, nc.scalar.copy)
 
         page_codes = {}
         page_scales = {}
 
         def quantise_page(b, c):
-            if b == 0 and c < 2:
-                codes = relay_tile("codes", last - 1 + c, c, BANK, U32)
+            if b == 0 and c < HELD_CHUNKS:
+                codes = relay_tile("first_codes%d" % c, LAST - 1 + c, c, BANK, U32)
             elif b == 0:
-                codes = held.tile([P, BANK], U32, name="ramp%d" % (last - 4 + c), align_bytes=64)
+                codes = held.tile([P, BANK], U32, name="ramp_then_codes%d" % (LAST - CHUNKS + c), align_bytes=64)
             else:
                 codes = held.tile([P, BANK], U32, name="page_codes%d" % c, align_bytes=64)
             scales = held.tile([P, BANK], U8, name="page_scales%d%d" % (b, c), align_bytes=64)
@@ -332,42 +354,43 @@ def tile_list_ramp_merge_forecast_kernel(
             page_codes[b, c] = codes
             page_scales[b, c] = scales
 
-        w4_codes = held.tile([P, H // PASS, 2 * N], U8, name="w4_codes", align_bytes=64)
-        w4_planes = held.tile([P, H // PASS, N], U8, name="w4_planes", align_bytes=64)
+        w4_codes = held.tile([P, R_PASSES, 2 * N], U8, name="w4_codes", align_bytes=64)
+        w4_scale_rows = held.tile([P, R_PASSES, N], U8, name="w4_scale_rows", align_bytes=64)
 
         def load_w4():
-            nc.gpsimd.memset(w4_planes[:], 0)
+            nc.vector.memset(w4_scale_rows[:].bitcast(I32), 0)
             nc.sync.dma_start(w4_codes[:].bitcast(I32), w4_words.rearrange("a p c -> p a c").bitcast(I32))
             for q in range(QUADS):
                 nc.sync.dma_start(
-                    w4_planes[QUAD * q : QUAD * q + 4, :, :].bitcast(I32),
-                    w4_scales[:, 4 * q : 4 * q + 4, :].rearrange("a r n -> r a n").bitcast(I32),
+                    w4_scale_rows[QUAD * q : QUAD * q + SCALE_ROWS, :, :].bitcast(I32),
+                    w4_scales[:, SCALE_ROWS * q : SCALE_ROWS * (q + 1), :].rearrange("a r n -> r a n").bitcast(I32),
                 )
 
         scores = {}
 
         def second_product(b, c, n):
             if b == 0:
-                scores[c, n] = bank((N_TILES * c + n) % 8)
+                scores[c, n] = bank((N_TILES * c + n) % BANKS)
             nc.tensor.matmul_mx(
                 scores[c, n][:],
                 lhsT=w4_codes[:, b, 2 * P * n : 2 * P * (n + 1)].bitcast(FP4X4),
-                lhsT_scale=w4_planes[:, b, P * n : P * (n + 1)],
+                lhsT_scale=w4_scale_rows[:, b, P * n : P * (n + 1)],
                 rhs=page_codes[b, c][:].bitcast(FP8X4),
                 rhs_scale=page_scales[b, c][:],
                 start=(b == 0),
-                stop=(b == H // PASS - 1),
+                stop=(b == R_PASSES - 1),
             )
 
         def store(c, n, copy):
-            staged = (spare if c < 2 else shared).tile(
-                [P, BANK], F32, name="staged%d%d" % (c, n), offset=((N_TILES * c + n) % 8) * BANK * 4
+            staged = (spare if c < HELD_CHUNKS else shared).tile(
+                [P, BANK], F32, name="staged%d%d" % (c, n), offset=((N_TILES * c + n) % BANKS) * BANK * 4
             )
             copy(staged[:], scores[c, n][:])
             nc.sync.dma_start(out[P * n : P * (n + 1), BANK * c : BANK * (c + 1)], staged[:])
 
-        hs = {}
         put_first_tile()
+        quantise_w1_plain(w1_tile1, P, 2 * P, nc.scalar.copy)
+
         for i in range(ROW_TILES):
             if i + 2 < ROW_TILES:
                 pages[i + 2] = load_page(i + 2)
@@ -377,56 +400,52 @@ def tile_list_ramp_merge_forecast_kernel(
                 load_second_pass_constants()
                 load_w4()
             if i == 0:
-                hs[1] = states(1, lambda: None)
-                for a in range(PASSES):
-                    quantise_w1_plain(a, w1_rest[a], W1_LEAD, PASS, nc.scalar.copy)
-            elif i < last:
-                hs[i + 1] = states(i + 1, lambda: scale_low(i - 1))
-                if i == 1:
-                    for a in range(PASSES):
-                        quantise_w1_dealt(a, w1_dealt[a])
+                h_next = states(1, lambda: None)
+                quantise_w1_plain(w1_rest, 2 * P, PASS, nc.scalar.copy)
+            elif i < LAST:
+                h_next = states(i + 1, lambda: scale_low(i - 1))
             else:
                 scale_low(i - 1)
-            if 2 <= i < last:
-                round_finished(i - 2)
-            if i == last - 2:
+            if i + 1 == W1_DEALT_AFTER:
+                quantise_w1_dealt(w1_upper)
+            if ROUND_LAG <= i + 1 <= LAST:
+                round_finished(i + 1 - ROUND_LAG)
+            if i == LAST - 2:
                 for c in (2, 3, 1):
                     weave_first_pass(c)
-            if i == last - 1:
+            if i == LAST - 1:
                 weave_first_pass(0)
             fetch(i)
             if i > 0:
                 put_sum(i - 1)
             minimum(i)
-            if i < last:
-                nc.vector.tensor_tensor(
-                    pages[i + 1][:].indirect(list2[:]), hs[i + 1][:], wgs_of(i + 1), ALU.mult
-                )
+            if i < LAST:
+                put_states(i + 1, h_next)
             else:
                 scale_low(i)
                 quantise_page(0, 0)
             put_low(i)
-            if i >= last - 1:
+            if i >= LAST - 1:
                 round_finished(i - 1)
-            if i in (last - 2, last - 1):
-                quantise_page(0, i - last + 4)
+            if i in (LAST - 2, LAST - 1):
+                quantise_page(0, i + CHUNKS - LAST)
         quantise_page(0, 1)
-        put_sum(last)
-        for c in range(2):
+        put_sum(LAST)
+
+        for c in range(HELD_CHUNKS):
             for n in range(N_TILES):
                 second_product(0, c, n)
 
-        round_page(last, 0, nc.vector.tensor_copy)
-        round_page(last, 1, nc.vector.tensor_copy)
-        round_page(last, 3, nc.scalar.copy)
+        round_into_woven(LAST, 0, nc.vector.tensor_copy)
+        round_into_woven(LAST, 1, nc.vector.tensor_copy)
+        round_into_woven(LAST, 3, nc.scalar.copy)
         quantise_page(1, 0)
-        round_page(last, 2, nc.vector.tensor_copy)
-        quantise_page(1, 1)
-        quantise_page(1, 2)
-        quantise_page(1, 3)
+        round_into_woven(LAST, 2, nc.vector.tensor_copy)
+        for c in range(1, CHUNKS):
+            quantise_page(1, c)
         for c in range(CHUNKS):
             for n in range(N_TILES):
-                if c >= 2:
+                if c >= HELD_CHUNKS:
                     second_product(0, c, n)
                 second_product(1, c, n)
-                store(c, n, nc.vector.tensor_copy if c >= 2 and n % 2 == 1 else nc.scalar.copy)
+                store(c, n, nc.vector.tensor_copy if c >= HELD_CHUNKS and n % 2 == 1 else nc.scalar.copy)

@@ -36,6 +36,8 @@ SCALE_ROWS = 4
 LIST_ROWS = 16
 PAGE_SLOTS = 5
 RELAYS = 3
+W1_LEAD = 2 * P
+FIRST_PIECES = 4
 ROUND_LAG = 3
 W1_DEALT_AFTER = 2
 ROW_ORDER = [(0, t) for t in range(PACK)] + [(1, t) for t in (2, 0, 1, 3)]
@@ -73,13 +75,15 @@ def tile_list_ramp_merge_forecast_kernel(
         list2 = held.tile([P, S // LIST_ROWS], U16, name="list2")
         list3 = held.tile([P, PAIRS // LIST_ROWS], U16, name="list3")
         list4 = held.tile([P, PAIRS // LIST_ROWS], U16, name="list4")
-        table = [shared.tile([P, T], I32, name="table%d" % a, offset=a * T * 4, align_bytes=64) for a in range(K_PASSES)]
+        table = [
+            shared.tile([P, T], I32, name="table%d" % a, offset=a * T * 4, align_bytes=64) for a in range(K_PASSES)
+        ]
         table_scales = held.tile([P, T], U8, name="table_scales", align_bytes=64)
         nc.vector.memset(table_scales[:].bitcast(I32), 0)
         nc.sync.dma_start(list1[:], offs)
         nc.sync.dma_start(table[0][:], tab_words[0].rearrange("p n t -> p (n t)").bitcast(I32))
         for q in range(QUADS):
-            nc.gpsimd.dma_start(
+            nc.sync.dma_start(
                 table_scales[QUAD * q : QUAD * q + SCALE_ROWS * K_PASSES, :].bitcast(I32),
                 tab_scales[:, SCALE_ROWS * q : SCALE_ROWS * (q + 1), :].bitcast(I32),
             )
@@ -113,7 +117,7 @@ def tile_list_ramp_merge_forecast_kernel(
             nc.sync.dma_start(tile[:], rows_of(page0, i))
             return tile
 
-        w1_tile0 = load_w1(spare, 0, 0, P)
+        w1_lead = load_w1(spare, 0, 0, W1_LEAD)
         nc.sync.dma_start(table[1][:], tab_words[1].rearrange("p n t -> p (n t)").bitcast(I32))
         gains = [held.tile([P, PACK], F32, name="gains%d" % b) for b in range(R_PASSES)]
         backs = [held.tile([P, PACK], F32, name="backs%d" % b) for b in range(R_PASSES)]
@@ -121,16 +125,15 @@ def tile_list_ramp_merge_forecast_kernel(
         nc.scalar.dma_start(first_gain[:], gain[0:P].rearrange("(p t) -> p t", t=1))
         wgs_plain = held.tile([P, S], F32, name="wgs_plain")
         wgs_dealt = held.tile([P, PACK, S], F32, name="wgs_dealt")
-        conds = {0: load_cond(0)}
         nc.sync.dma_start(wgs_plain[:, 0:BANK], wgs[:, 0:BANK])
+        conds = {0: load_cond(0)}
         nc.sync.dma_start(list2[:], offs2)
         pages = {0: load_page(0)}
-        w1_tile1 = load_w1(spare, 0, P, 2 * P)
         nc.sync.dma_start(wgs_plain[:, BANK:S], wgs[:, BANK:S])
         conds[1] = load_cond(1)
         with nc.allow_non_contiguous_dma(reason="one value of a channel vector for each partition"):
             nc.sync.dma_start(gains[0][:, 1:PACK], gain[P:PASS].rearrange("(t p) -> p t", p=P))
-        w1_rest = load_w1(spare, 0, 2 * P, PASS)
+        w1_rest = load_w1(spare, 0, W1_LEAD, PASS)
         nc.sync.dma_start(list3[:], offs3)
         nc.sync.dma_start(list4[:], offs4)
         pages[1] = load_page(1)
@@ -188,7 +191,7 @@ def tile_list_ramp_merge_forecast_kernel(
                     w1_codes[a, 1][:].bitcast(FP8X4), w1_scales[a, 1][:], w1_woven[:].rearrange("p t m j -> p (t m j)")
                 )
 
-        quantise_w1_plain(w1_tile0, 0, P, nc.vector.tensor_copy)
+        quantise_w1_plain(w1_lead, 0, W1_LEAD, nc.vector.tensor_copy)
         for half in range(HALVES):
             nc.vector.tensor_copy(
                 picked[1][:, BANK * half : BANK * (half + 1)],
@@ -275,8 +278,8 @@ def tile_list_ramp_merge_forecast_kernel(
         mains, ramps, lows, back_lows = {}, {}, {}, {}
 
         def fetch(i):
-            mains[i] = relay_tile("main%d" % i, i if i > 0 else -1, 0, PAIRS, F32)
-            tag = "ramp_then_codes%d" % i if i in (LAST - 2, LAST - 1) else "ramp"
+            mains[i] = relay_tile("main%d" % i, i, 0, PAIRS, F32)
+            tag = "ramp_then_codes" if i == LAST - 2 else "ramp"
             ramps[i] = held.tile([P, PAIRS], F32, name=tag, align_bytes=64)
             nc.vector.tensor_copy(mains[i][:], pages[i][:].indirect(list3[:]))
             nc.vector.tensor_copy(ramps[i][:], pages[i][:].indirect(list4[:]))
@@ -299,9 +302,11 @@ def tile_list_ramp_merge_forecast_kernel(
         def put_sum(i):
             nc.vector.tensor_tensor(pages[i][:].indirect(list4[:]), mains[i][:], back_lows[i][:], ALU.add)
 
-        def round_into_woven(i, c, cast):
+        def round_into_woven(i, c, cast, pieces=1):
             b, t = ROW_ORDER[i]
-            cast(woven[b, c][:, :, t], pages[i][:, BANK * c : BANK * (c + 1)])
+            width = BANK // pieces
+            for c0 in range(0, BANK, width):
+                cast(woven[b, c][:, c0 : c0 + width, t], pages[i][:, BANK * c + c0 : BANK * c + c0 + width])
 
         def round_and_deal(i):
             rounded = held.tile([P, T2], BF16, name=product_tag(i + ROUND_LAG), align_bytes=64)
@@ -342,15 +347,24 @@ def tile_list_ramp_merge_forecast_kernel(
         page_codes = {}
         page_scales = {}
 
-        def quantise_page(b, c):
-            if b == 0 and c < HELD_CHUNKS:
-                codes = relay_tile("first_codes%d" % c, LAST - 1 + c, c, BANK, U32)
-            elif b == 0:
-                codes = held.tile([P, BANK], U32, name="ramp_then_codes%d" % (LAST - CHUNKS + c), align_bytes=64)
+        def quantise_page(b, c, pieces=1):
+            if (b, c) == (0, 0):
+                codes = relay_tile("first_codes0", LAST, 1, BANK, U32)
+            elif (b, c) == (0, 1):
+                codes = held.tile([P, BANK], U32, name="ramp", align_bytes=64)
+            elif (b, c) == (0, 2):
+                codes = held.tile([P, BANK], U32, name="ramp_then_codes", align_bytes=64)
+            elif (b, c) == (0, 3):
+                codes = relay_tile("first_codes3", LAST - 1, 0, BANK, U32)
             else:
                 codes = held.tile([P, BANK], U32, name="page_codes%d" % c, align_bytes=64)
             scales = held.tile([P, BANK], U8, name="page_scales%d%d" % (b, c), align_bytes=64)
-            nc.vector.quantize_mx(codes[:].bitcast(FP8X4), scales[:], woven[b, c][:].rearrange("p c t -> p (c t)"))
+            width = BANK // pieces
+            for c0 in range(0, BANK, width):
+                cols = slice(c0, c0 + width)
+                nc.vector.quantize_mx(
+                    codes[:, cols].bitcast(FP8X4), scales[:, cols], woven[b, c][:, cols, :].rearrange("p c t -> p (c t)")
+                )
             page_codes[b, c] = codes
             page_scales[b, c] = scales
 
@@ -358,7 +372,7 @@ def tile_list_ramp_merge_forecast_kernel(
         w4_scale_rows = held.tile([P, R_PASSES, N], U8, name="w4_scale_rows", align_bytes=64)
 
         def load_w4():
-            nc.vector.memset(w4_scale_rows[:].bitcast(I32), 0)
+            nc.gpsimd.memset(w4_scale_rows[:], 0)
             nc.sync.dma_start(w4_codes[:].bitcast(I32), w4_words.rearrange("a p c -> p a c").bitcast(I32))
             for q in range(QUADS):
                 nc.sync.dma_start(
@@ -389,7 +403,6 @@ def tile_list_ramp_merge_forecast_kernel(
             nc.sync.dma_start(out[P * n : P * (n + 1), BANK * c : BANK * (c + 1)], staged[:])
 
         put_first_tile()
-        quantise_w1_plain(w1_tile1, P, 2 * P, nc.scalar.copy)
 
         for i in range(ROW_TILES):
             if i + 2 < ROW_TILES:
@@ -401,7 +414,7 @@ def tile_list_ramp_merge_forecast_kernel(
                 load_w4()
             if i == 0:
                 h_next = states(1, lambda: None)
-                quantise_w1_plain(w1_rest, 2 * P, PASS, nc.scalar.copy)
+                quantise_w1_plain(w1_rest, W1_LEAD, PASS, nc.scalar.copy)
             elif i < LAST:
                 h_next = states(i + 1, lambda: scale_low(i - 1))
             else:
@@ -423,25 +436,26 @@ def tile_list_ramp_merge_forecast_kernel(
                 put_states(i + 1, h_next)
             else:
                 scale_low(i)
-                quantise_page(0, 0)
+                quantise_page(0, 3)
             put_low(i)
             if i >= LAST - 1:
                 round_finished(i - 1)
-            if i in (LAST - 2, LAST - 1):
-                quantise_page(0, i + CHUNKS - LAST)
-        quantise_page(0, 1)
+            if i == LAST - 2:
+                quantise_page(0, 2)
+        for c in range(HELD_CHUNKS):
+            quantise_page(0, c)
         put_sum(LAST)
 
         for c in range(HELD_CHUNKS):
             for n in range(N_TILES):
                 second_product(0, c, n)
 
-        round_into_woven(LAST, 0, nc.vector.tensor_copy)
+        round_into_woven(LAST, 0, nc.vector.tensor_copy, pieces=FIRST_PIECES)
+        quantise_page(1, 0, pieces=FIRST_PIECES)
         round_into_woven(LAST, 1, nc.vector.tensor_copy)
-        round_into_woven(LAST, 3, nc.scalar.copy)
-        quantise_page(1, 0)
-        round_into_woven(LAST, 2, nc.vector.tensor_copy)
         for c in range(1, CHUNKS):
+            if c + 1 < CHUNKS:
+                round_into_woven(LAST, c + 1, nc.vector.tensor_copy)
             quantise_page(1, c)
         for c in range(CHUNKS):
             for n in range(N_TILES):

from contextlib import ExitStack

import concourse.mybir as mybir
from concourse.masks import make_identity

K, H, N, T, S, T2, PAIRS = 1024, 1024, 512, 4096, 1024, 2048, 512
FLOPS = 2 * K * H * S + 2 * H * N * T2

F32 = mybir.dt.float32
BF16 = mybir.dt.bfloat16
I32 = mybir.dt.int32
U32 = mybir.dt.uint32
U16 = mybir.dt.uint16
U8 = mybir.dt.uint8
FP8X4 = mybir.dt.float8_e4m3fn_x4
FP4X4 = mybir.dt.float4_e2m1fn_x4
ALU = mybir.AluOpType
ACT = mybir.ActivationFunctionType

P = 128
PACK = 4
PASS = P * PACK
BANK = 512
BANKS = 8
K_PASSES = K // PASS
R_PASSES = H // PASS
ROW_TILES = H // P
LAST = ROW_TILES - 1
CHUNKS = T2 // BANK
HELD_CHUNKS = BANKS * P // N
HALVES = S // BANK
N_TILES = N // P
QUADS = 4
QUAD = P // QUADS
SCALE_ROWS = 4
LIST_ROWS = 16
PAGE_SLOTS = 5
RELAYS = 3
W1_LEAD = 2 * P
FIRST_PIECES = 4
ROUND_LAG = 3
W1_DEALT_AFTER = 2
ROW_ORDER = [(0, t) for t in range(PACK)] + [(1, t) for t in (2, 0, 1, 3)]


def tile_list_ramp_merge_forecast_kernel(
    tc, tab_words, tab_scales, offs, w1, cond, gain, page0, wgs, offs2, offs3, offs4, back, w4_words, w4_scales, out
):
    nc = tc.nc
    with ExitStack() as ctx:
        held = ctx.enter_context(tc.tile_pool(name="held", bufs=1))
        shared = ctx.enter_context(tc.tile_pool(name="shared", bufs=1))
        relay = ctx.enter_context(tc.tile_pool(name="relay", bufs=1))
        ring2 = ctx.enter_context(tc.tile_pool(name="ring2", bufs=2))
        ring3 = ctx.enter_context(tc.tile_pool(name="ring3", bufs=3))
        spare = ctx.enter_context(tc.tile_pool(name="spare", bufs=1))
        psum = ctx.enter_context(tc.psum_pool(name="psum", bufs=1))

        def bank(index):
            return psum.tile([P, BANK], F32, name="bank%d" % index, offset=index * BANK * 4)

        def bank_pair():
            return psum.tile([P, S], F32, name="bank_pair", offset=0)

        def rows_of(matrix, i):
            b, t = ROW_ORDER[i]
            if b == 0:
                return matrix[P * t : P * (t + 1), :]
            return matrix[PASS * b : PASS * (b + 1), :].rearrange("(p t) c -> t p c", t=PACK)[t]

        def list_half(entries, half):
            return entries[:, BANK // LIST_ROWS * half : BANK // LIST_ROWS * (half + 1)]

        list1 = held.tile([P, S // LIST_ROWS], U16, name="list1")
        list2 = held.tile([P, S // LIST_ROWS], U16, name="list2")
        list3 = held.tile([P, PAIRS // LIST_ROWS], U16, name="list3")
        list4 = held.tile([P, PAIRS // LIST_ROWS], U16, name="list4")
        table = [
            shared.tile([P, T], I32, name="table%d" % a, offset=a * T * 4, align_bytes=64) for a in range(K_PASSES)
        ]
        table_scales = held.tile([P, T], U8, name="table_scales", align_bytes=64)
        nc.vector.memset(table_scales[:].bitcast(I32), 0)
        nc.sync.dma_start(list1[:], offs)
        nc.sync.dma_start(table[0][:], tab_words[0].rearrange("p n t -> p (n t)").bitcast(I32))
        for q in range(QUADS):
            nc.sync.dma_start(
                table_scales[QUAD * q : QUAD * q + SCALE_ROWS * K_PASSES, :].bitcast(I32),
                tab_scales[:, SCALE_ROWS * q : SCALE_ROWS * (q + 1), :].bitcast(I32),
            )

        def load_w1(pool, start, c0, c1):
            tiles = []
            for a in range(K_PASSES):
                offset = start + (a * PASS + c0 % PASS) * PACK * 4
                raw = pool.tile([P, PACK, c1 - c0], F32, name="w1_raw%d_%d" % (a, c0), offset=offset)
                nc.sync.dma_start(raw[:], w1[PASS * a : PASS * (a + 1), c0:c1].rearrange("(p j) c -> p j c", j=PACK))
                tiles.append(raw)
            return tiles

        def product_tag(i):
            if i == W1_DEALT_AFTER:
                return "product_then_w1"
            return "even_planes" if i == LAST else "product_%d" % (i % 2)

        def load_cond(i):
            if i == W1_DEALT_AFTER:
                tile = held.tile([P, S], F32, name="cond_then_w1", align_bytes=64)
            elif i == LAST:
                tile = held.tile([P, S], F32, name="cond_then_woven", align_bytes=64)
            else:
                tile = ring2.tile([P, S], F32, name="cond_rows")
            nc.sync.dma_start(tile[:], rows_of(cond, i))
            return tile

        def load_page(i):
            tile = held.tile([P, T2], F32, name="page%d" % (i % PAGE_SLOTS))
            nc.sync.dma_start(tile[:], rows_of(page0, i))
            return tile

        w1_lead = load_w1(spare, 0, 0, W1_LEAD)
        nc.sync.dma_start(table[1][:], tab_words[1].rearrange("p n t -> p (n t)").bitcast(I32))
        gains = [held.tile([P, PACK], F32, name="gains%d" % b) for b in range(R_PASSES)]
        backs = [held.tile([P, PACK], F32, name="backs%d" % b) for b in range(R_PASSES)]
        first_gain = held.tile([P, 1], F32, name="first_gain")
        nc.scalar.dma_start(first_gain[:], gain[0:P].rearrange("(p t) -> p t", t=1))
        wgs_plain = held.tile([P, S], F32, name="wgs_plain")
        wgs_dealt = held.tile([P, PACK, S], F32, name="wgs_dealt")
        nc.sync.dma_start(wgs_plain[:, 0:BANK], wgs[:, 0:BANK])
        conds = {0: load_cond(0)}
        nc.sync.dma_start(list2[:], offs2)
        pages = {0: load_page(0)}
        nc.sync.dma_start(wgs_plain[:, BANK:S], wgs[:, BANK:S])
        conds[1] = load_cond(1)
        with nc.allow_non_contiguous_dma(reason="one value of a channel vector for each partition"):
            nc.sync.dma_start(gains[0][:, 1:PACK], gain[P:PASS].rearrange("(t p) -> p t", p=P))
        w1_rest = load_w1(spare, 0, W1_LEAD, PASS)
        nc.sync.dma_start(list3[:], offs3)
        nc.sync.dma_start(list4[:], offs4)
        pages[1] = load_page(1)
        with nc.allow_non_contiguous_dma(reason="one value of a channel vector for each partition"):
            nc.sync.dma_start(backs[0][:], back[0:PASS].rearrange("(t p) -> p t", p=P))
        conds[2] = load_cond(2)
        w1_upper = load_w1(shared, T * 4, PASS, H)

        def load_second_pass_constants():
            nc.sync.dma_start(gains[1][:], gain[PASS:H].rearrange("(p t) -> p t", t=PACK))
            nc.sync.dma_start(backs[1][:], back[PASS:H].rearrange("(p t) -> p t", t=PACK))
            for q in range(QUADS):
                nc.sync.dma_start(wgs_dealt[QUAD * q : QUAD * (q + 1), :, :], wgs.rearrange("(m t) j -> m t j", t=PACK))

        def wgs_of(i):
            b, t = ROW_ORDER[i]
            return wgs_plain[:] if b == 0 else wgs_dealt[:, t, :]

        identity = held.tile([P, P], F32, name="identity")
        make_identity(nc, identity[:])

        picked = [held.tile([P, S], U32, name="picked%d" % a, align_bytes=64) for a in range(K_PASSES)]
        picked_scales = held.tile([P, S], U8, name="picked_scales", align_bytes=64)
        nc.vector.tensor_copy(picked[0][:], table[0][:].bitcast(U32).indirect(list1[:]))
        nc.vector.tensor_copy(picked_scales[:], table_scales[:].indirect(list1[:]))

        w1_codes = {}
        w1_scales = {}
        for a in range(K_PASSES):
            for b in range(R_PASSES):
                w1_codes[a, b] = held.tile([P, PASS], U32, name="w1_codes%d%d" % (a, b), align_bytes=64)
                w1_scales[a, b] = held.tile([P, PASS], U8, name="w1_scales%d%d" % (a, b), align_bytes=64)

        def quantise_w1_plain(raws, c0, c1, cast):
            for a, raw in enumerate(raws):
                w1_woven = ring2.tile([P, c1 - c0, PACK], BF16, name="w1_woven", align_bytes=64)
                cast(
                    w1_woven[:].rearrange("p (c e) j -> p c j e", e=PACK),
                    raw[:].rearrange("p j (c e) -> p c j e", e=PACK),
                )
                nc.vector.quantize_mx(
                    w1_codes[a, 0][:, c0:c1].bitcast(FP8X4),
                    w1_scales[a, 0][:, c0:c1],
                    w1_woven[:].rearrange("p c j -> p (c j)"),
                )

        def quantise_w1_dealt(raws):
            for a, raw in enumerate(raws):
                tag = ("cond_then_w1", "product_then_w1")[a]
                w1_woven = held.tile([P, PACK, P, PACK], BF16, name=tag, align_bytes=64)
                nc.scalar.copy(
                    w1_woven[:].rearrange("p t m j -> p m t j"), raw[:].rearrange("p j (m t) -> p m t j", t=PACK)
                )
                nc.vector.quantize_mx(
                    w1_codes[a, 1][:].bitcast(FP8X4), w1_scales[a, 1][:], w1_woven[:].rearrange("p t m j -> p (t m j)")
                )

        quantise_w1_plain(w1_lead, 0, W1_LEAD, nc.vector.tensor_copy)
        for half in range(HALVES):
            nc.vector.tensor_copy(
                picked[1][:, BANK * half : BANK * (half + 1)],
                table[1][:].bitcast(U32).indirect(list_half(list1, half)),
            )

        def first_product(i, half, acc):
            b, t = ROW_ORDER[i]
            cols = slice(BANK * half, BANK * (half + 1))
            for a in range(K_PASSES):
                nc.tensor.matmul_mx(
                    acc[:, cols],
                    lhsT=w1_codes[a, b][:, P * t : P * (t + 1)].bitcast(FP8X4),
                    lhsT_scale=w1_scales[a, b][:, P * t : P * (t + 1)],
                    rhs=picked[a][:, cols].bitcast(FP8X4),
                    rhs_scale=picked_scales[SCALE_ROWS * a : P, cols],
                    start=(a == 0),
                    stop=(a == K_PASSES - 1),
                )

        def relay_tile(name, step, part, width, dtype):
            offset = ((step % RELAYS) * S + part * PAIRS) * 4
            return relay.tile([P, width], dtype, name=name, offset=offset, align_bytes=64)

        def states(i, between):
            b, t = ROW_ORDER[i]
            h = ring3.tile([P, S], F32, name="h")
            silu_turned = relay_tile("silu_turned%d" % i, i - 1, 0, S, F32)
            product = held.tile([P, S], F32, name=product_tag(i), align_bytes=64)
            acc = bank_pair()
            for half in range(HALVES):
                cols = slice(BANK * half, BANK * (half + 1))
                first_product(i, half, acc)
                nc.scalar.copy(product[:, cols], acc[:, cols])
            for half in range(HALVES):
                cols = slice(BANK * half, BANK * (half + 1))
                turned = bank(HALVES + half)
                for q in range(BANK // P):
                    block = slice(P * q, P * (q + 1))
                    source = slice(BANK * half + P * q, BANK * half + P * (q + 1))
                    nc.tensor.matmul(
                        turned[:, block], conds[i][:, source], identity[:], start=True, stop=False, is_transpose=True
                    )
                    nc.tensor.matmul(
                        turned[:, block], product[:, source], identity[:], start=False, stop=True, is_transpose=True
                    )
                nc.scalar.activation(silu_turned[:, cols], turned[:], ACT.Silu)
            upright = bank_pair()
            for half in range(HALVES):
                cols = slice(BANK * half, BANK * (half + 1))
                for q in range(BANK // P):
                    block = slice(BANK * half + P * q, BANK * half + P * (q + 1))
                    nc.tensor.transpose(upright[:, block], silu_turned[:, block], identity[:])
                if half == HALVES - 1:
                    between()
                nc.scalar.activation(h[:, cols], upright[:, cols], ACT.Copy, scale=gains[b][:, t : t + 1])
            return h

        def put_first_tile():
            gained = ring3.tile([P, S], F32, name="h")
            silu = held.tile([P, S], F32, name="even_planes", align_bytes=64)
            acc = bank_pair()
            pre = held.tile([P, S], F32, name=product_tag(0), align_bytes=64)
            nc.vector.tensor_scalar(gained[:, 0:BANK], wgs_plain[:, 0:BANK], first_gain[:], None, ALU.mult)
            for half in range(HALVES):
                cols = slice(BANK * half, BANK * (half + 1))
                first_product(0, half, acc)
                nc.vector.tensor_tensor(pre[:, cols], acc[:, cols], conds[0][:, cols], ALU.add)
                nc.scalar.activation(silu[:, cols], pre[:, cols], ACT.Silu)
            nc.scalar.activation(gained[:, BANK:S], wgs_plain[:, BANK:S], ACT.Copy, scale=first_gain[:])
            for half in range(HALVES):
                cols = slice(BANK * half, BANK * (half + 1))
                window = pages[0][:].indirect(list_half(list2, half))
                nc.vector.tensor_tensor(window, silu[:, cols], gained[:, cols], ALU.mult)

        woven = {}
        for c in range(CHUNKS):
            woven[1, c] = shared.tile(
                [P, BANK, PACK], BF16, name="woven%d" % c, offset=T * 4 + c * BANK * PACK * 2, align_bytes=64
            )
        planes = shared.tile([P, PACK, T2], BF16, name="planes", offset=0, align_bytes=64)
        even_planes = held.tile([P, 2, T2], BF16, name="even_planes", align_bytes=64)

        mains, ramps, lows, back_lows = {}, {}, {}, {}

        def fetch(i):
            mains[i] = relay_tile("main%d" % i, i, 0, PAIRS, F32)
            tag = "ramp_then_codes" if i == LAST - 2 else "ramp"
            ramps[i] = held.tile([P, PAIRS], F32, name=tag, align_bytes=64)
            nc.vector.tensor_copy(mains[i][:], pages[i][:].indirect(list3[:]))
            nc.vector.tensor_copy(ramps[i][:], pages[i][:].indirect(list4[:]))

        def minimum(i):
            lows[i] = held.tile([P, PAIRS], F32, name="low")
            nc.vector.tensor_tensor(lows[i][:], mains[i][:], ramps[i][:], ALU.min)

        def scale_low(i):
            b, t = ROW_ORDER[i]
            back_lows[i] = relay_tile("back_low%d" % i, i + 1, 1, PAIRS, F32)
            nc.scalar.activation(back_lows[i][:], lows[i][:], ACT.Copy, scale=backs[b][:, t : t + 1])

        def put_states(i, h):
            nc.vector.tensor_tensor(pages[i][:].indirect(list2[:]), h[:], wgs_of(i), ALU.mult)

        def put_low(i):
            nc.vector.tensor_copy(pages[i][:].indirect(list3[:]), lows[i][:])

        def put_sum(i):
            nc.vector.tensor_tensor(pages[i][:].indirect(list4[:]), mains[i][:], back_lows[i][:], ALU.add)

        def round_into_woven(i, c, cast, pieces=1):
            b, t = ROW_ORDER[i]
            width = BANK // pieces
            for c0 in range(0, BANK, width):
                cast(woven[b, c][:, c0 : c0 + width, t], pages[i][:, BANK * c + c0 : BANK * c + c0 + width])

        def round_and_deal(i):
            rounded = held.tile([P, T2], BF16, name=product_tag(i + ROUND_LAG), align_bytes=64)
            nc.scalar.copy(rounded[:], pages[i][:])
            for t in range(PACK):
                nc.sync.dma_start(planes[QUAD * i : QUAD * (i + 1), t, :], rounded[t:P:PACK, :])

        def weave_first_pass(c):
            if c == 0:
                woven[0, c] = held.tile([P, BANK, PACK], BF16, name="cond_then_woven", align_bytes=64)
            else:
                woven[0, c] = spare.tile(
                    [P, BANK, PACK], BF16, name="woven_first%d" % c, offset=c * BANK * PACK * 2, align_bytes=64
                )
            nc.scalar.copy(
                woven[0, c][:].rearrange("p (c e) t -> p c t e", e=PACK),
                planes[:, :, BANK * c : BANK * (c + 1)].rearrange("p t (c e) -> p c t e", e=PACK),
            )

        def weave_even_planes(c):
            nc.scalar.copy(
                woven[1, c][:, :, 0:PACK:2], even_planes[:, :, BANK * c : BANK * (c + 1)].rearrange("p e c -> p c e")
            )

        def round_finished(i):
            b, t = ROW_ORDER[i]
            if b == 0:
                round_and_deal(i)
            elif t % 2 == 0:
                nc.scalar.copy(even_planes[:, t // 2, :], pages[i][:])
                if t == 0:
                    for c in range(CHUNKS):
                        weave_even_planes(c)
            else:
                for c in range(CHUNKS):
                    round_into_woven(i, c, nc.scalar.copy)

        page_codes = {}
        page_scales = {}

        def quantise_page(b, c, pieces=1):
            if (b, c) == (0, 0):
                codes = relay_tile("first_codes0", LAST, 1, BANK, U32)
            elif (b, c) == (0, 1):
                codes = held.tile([P, BANK], U32, name="ramp", align_bytes=64)
            elif (b, c) == (0, 2):
                codes = held.tile([P, BANK], U32, name="ramp_then_codes", align_bytes=64)
            elif (b, c) == (0, 3):
                codes = relay_tile("first_codes3", LAST - 1, 0, BANK, U32)
            else:
                codes = held.tile([P, BANK], U32, name="page_codes%d" % c, align_bytes=64)
            scales = held.tile([P, BANK], U8, name="page_scales%d%d" % (b, c), align_bytes=64)
            width = BANK // pieces
            for c0 in range(0, BANK, width):
                cols = slice(c0, c0 + width)
                nc.vector.quantize_mx(
                    codes[:, cols].bitcast(FP8X4), scales[:, cols], woven[b, c][:, cols, :].rearrange("p c t -> p (c t)")
                )
            page_codes[b, c] = codes
            page_scales[b, c] = scales

        w4_codes = held.tile([P, R_PASSES, 2 * N], U8, name="w4_codes", align_bytes=64)
        w4_scale_rows = held.tile([P, R_PASSES, N], U8, name="w4_scale_rows", align_bytes=64)

        def load_w4():
            nc.gpsimd.memset(w4_scale_rows[:], 0)
            nc.sync.dma_start(w4_codes[:].bitcast(I32), w4_words.rearrange("a p c -> p a c").bitcast(I32))
            for q in range(QUADS):
                nc.sync.dma_start(
                    w4_scale_rows[QUAD * q : QUAD * q + SCALE_ROWS, :, :].bitcast(I32),
                    w4_scales[:, SCALE_ROWS * q : SCALE_ROWS * (q + 1), :].rearrange("a r n -> r a n").bitcast(I32),
                )

        scores = {}

        def second_product(b, c, n):
            if b == 0:
                scores[c, n] = bank((N_TILES * c + n) % BANKS)
            nc.tensor.matmul_mx(
                scores[c, n][:],
                lhsT=w4_codes[:, b, 2 * P * n : 2 * P * (n + 1)].bitcast(FP4X4),
                lhsT_scale=w4_scale_rows[:, b, P * n : P * (n + 1)],
                rhs=page_codes[b, c][:].bitcast(FP8X4),
                rhs_scale=page_scales[b, c][:],
                start=(b == 0),
                stop=(b == R_PASSES - 1),
            )

        def store(c, n, copy):
            staged = (spare if c < HELD_CHUNKS else shared).tile(
                [P, BANK], F32, name="staged%d%d" % (c, n), offset=((N_TILES * c + n) % BANKS) * BANK * 4
            )
            copy(staged[:], scores[c, n][:])
            nc.sync.dma_start(out[P * n : P * (n + 1), BANK * c : BANK * (c + 1)], staged[:])

        put_first_tile()

        for i in range(ROW_TILES):
            if i + 2 < ROW_TILES:
                pages[i + 2] = load_page(i + 2)
            if i + 3 < ROW_TILES:
                conds[i + 3] = load_cond(i + 3)
            if i == 1:
                load_second_pass_constants()
                load_w4()
            if i == 0:
                h_next = states(1, lambda: None)
                quantise_w1_plain(w1_rest, W1_LEAD, PASS, nc.scalar.copy)
            elif i < LAST:
                h_next = states(i + 1, lambda: scale_low(i - 1))
            else:
                scale_low(i - 1)
            if i + 1 == W1_DEALT_AFTER:
                quantise_w1_dealt(w1_upper)
            if ROUND_LAG <= i + 1 <= LAST:
                round_finished(i + 1 - ROUND_LAG)
            if i == LAST - 2:
                for c in (2, 3, 1):
                    weave_first_pass(c)
            if i == LAST - 1:
                weave_first_pass(0)
            fetch(i)
            if i > 0:
                put_sum(i - 1)
            minimum(i)
            if i < LAST:
                put_states(i + 1, h_next)
            else:
                scale_low(i)
                quantise_page(0, 3)
            put_low(i)
            if i >= LAST - 1:
                round_finished(i - 1)
            if i == LAST - 2:
                quantise_page(0, 2)
        for c in range(HELD_CHUNKS):
            quantise_page(0, c)
        put_sum(LAST)

        for c in range(HELD_CHUNKS):
            for n in range(N_TILES):
                second_product(0, c, n)

        round_into_woven(LAST, 0, nc.vector.tensor_copy, pieces=FIRST_PIECES)
        quantise_page(1, 0, pieces=FIRST_PIECES)
        round_into_woven(LAST, 1, nc.vector.tensor_copy)
        for c in range(1, CHUNKS):
            if c + 1 < CHUNKS:
                round_into_woven(LAST, c + 1, nc.vector.tensor_copy)
            quantise_page(1, c)
        for c in range(CHUNKS):
            for n in range(N_TILES):
                if c >= HELD_CHUNKS:
                    second_product(0, c, n)
                second_product(1, c, n)
                store(c, n, nc.vector.tensor_copy if c >= HELD_CHUNKS and n % 2 == 1 else nc.scalar.copy)
